import numpy as np
import ml_dtypes


def mxq(x, axis, fmt="e4m3"):
    dtype, down = {"e4m3": (ml_dtypes.float8_e4m3fn, 7), "e5m2": (ml_dtypes.float8_e5m2, 14)}[fmt]
    v = np.moveaxis(np.asarray(x, np.float32).astype(ml_dtypes.bfloat16).astype(np.float64), axis, -1)
    blocks = v.reshape(v.shape[:-1] + (-1, 32))
    amax = np.abs(blocks).max(-1, keepdims=True)
    byte = np.maximum(np.where(amax > 0, np.frexp(amax)[1] - 1 + 127, 0) - down, 1)
    scale = np.exp2(byte - 127.0)
    codes = (blocks / scale).astype(np.float32).astype(dtype).astype(np.float64)
    return np.moveaxis((codes * scale).reshape(v.shape), -1, axis)


WIDE = False


def mx_kscale(k):
    if not WIDE:
        return np.ones(k)
    levels = np.array([10, -10, 5, -5, 0])
    if k % 512:
        return np.exp2(np.random.permutation(np.resize(levels, k // 32))).repeat(32)
    a = np.empty((k // 512, 16))
    for p in range(k // 512):
        a[p, :8] = np.random.permutation(np.resize(levels, 8))
        for g in range(8):
            far = levels[np.abs(levels - a[p, g]) >= 10]
            a[p, g + 8] = far[np.random.randint(len(far))]
    return np.exp2(a.ravel()).repeat(32)


def f64(x):
    return np.asarray(x).astype(np.float64)


def striped(idx):
    return np.tile(idx.reshape(-1, 16).T, (8, 1)).astype(np.uint16)


def unstriped(offs):
    return offs[:16].T.reshape(-1).astype(np.int64)


def pack_weight(w):
    k, n = w.shape
    w = f64(np.asarray(w, np.float32).astype(ml_dtypes.bfloat16)).reshape(k // 32, 32, n)
    amax = np.abs(w).max(1)
    byte = np.clip(np.where(amax > 0, np.frexp(amax)[1] - 1 + 127 - 7, 1), 1, 254)
    scaled = (w * np.exp2(127.0 - byte)[:, None, :]).reshape(k, n).astype(np.float32)
    words = np.ascontiguousarray(scaled.reshape(k // 512, 128, 4, n).transpose(0, 1, 3, 2)).astype(ml_dtypes.float8_e4m3fn).view(np.uint8)
    return words, np.ascontiguousarray(byte.astype(np.uint8).reshape(k // 512, 16, n))


def unpack_weight(words, scales):
    g, p, n, _ = words.shape
    vals = np.ascontiguousarray(words).view(ml_dtypes.float8_e4m3fn).astype(np.float64) * np.repeat(np.exp2(scales.astype(np.float64) - 127.0), 8, axis=1)[..., None]
    return vals.transpose(0, 1, 3, 2).reshape(g * 512, n)


def silu(v):
    return v / (1.0 + np.exp(-np.maximum(v, -700.0)))


K, T, S, V, H, N, J, U = 1024, 2048, 512, 256, 512, 128, 512, 512


def setup_inputs():
    n = np.random.standard_normal
    s = mx_kscale(K)[:, None]
    u = mx_kscale(H)
    r = mx_kscale(J)[:, None]
    packed_xT = pack_weight(n((K, T)) * s)
    packed_w2 = pack_weight(n((H, N)) / np.sqrt(2 * H) / u[:, None])
    return {
        "x_words": packed_xT[0],
        "x_scales": packed_xT[1],
        "aT": (n((J, U)) * r).astype(np.float32),
        "w1": (n((K, H)) / np.sqrt(K) / s * u).astype(np.float32),
        "w3": (n((J, H)) / np.sqrt(J) / r).astype(np.float32),
        "w2_words": packed_w2[0],
        "w2_scales": packed_w2[1],
        "offs": striped(np.random.permutation(T)[:S]),
        "pos1": striped(np.random.permutation(S)[:V]),
        "pos2": striped(np.random.permutation(S)[:V]),
    }


def reference(x_words, x_scales, aT, w1, w3, w2_words, w2_scales, offs, pos1, pos2):
    xq = unpack_weight(x_words, x_scales)[:, unstriped(offs)]
    h = silu(mxq(f64(w1), 0, "e4m3").T @ xq)
    f = mxq(f64(w3), 0, "e4m3").T @ mxq(f64(aT), 0, "e4m3")
    z = h[:, unstriped(pos1)] * f[:, :V] + h[:, unstriped(pos2)] * f[:, V:2 * V]
    return silu(unpack_weight(w2_words, w2_scales).T @ mxq(z, 0, "e4m3"))

@@ -1,0 +1,232 @@
+from contextlib import ExitStack
+
+import concourse.mybir as mybir
+
+K, T, S, V, H, N, J = 1024, 2048, 512, 256, 512, 128, 512
+FLOPS = 2 * K * H * S + 2 * J * H * 2 * V + 2 * H * N * V
+
+F32 = mybir.dt.float32
+BF16 = mybir.dt.bfloat16
+I32 = mybir.dt.int32
+U32 = mybir.dt.uint32
+U16 = mybir.dt.uint16
+U8 = mybir.dt.uint8
+FP8X4 = mybir.dt.float8_e4m3fn_x4
+SILU = mybir.ActivationFunctionType.Silu
+MULT = mybir.AluOpType.mult
+ADD = mybir.AluOpType.add
+
+P = 128
+PACK = 4
+K_PASS = P * PACK
+PASSES = K // K_PASS
+D = 2
+
+
+def tile_picked_dime_silu_p_kernel(
+    tc, x_words, x_scales, aT, w1, w3, w2_words, w2_scales, offs, pos1, pos2, out
+):
+    nc = tc.nc
+    with ExitStack() as ctx:
+        sb = ctx.enter_context(tc.tile_pool(name="sb", bufs=1))
+        psum = ctx.enter_context(tc.psum_pool(name="psum", bufs=1))
+
+        def tile(name, shape, dtype, tag=None):
+            return sb.tile(shape, dtype, name=name, tag=tag or name, align_bytes=64)
+
+        def quantise(name, grouped):
+            width = grouped.shape[1] // PACK
+            codes = tile(name + "_codes", [P, width], U32)
+            scales = tile(name + "_scales", [P, width], U8)
+            nc.vector.quantize_mx(out=codes[:].bitcast(FP8X4), scales=scales[:], in_=grouped)
+            return codes, scales
+
+        x_sc = tile("x_sc", [P, T], U8)
+        w2_sc = tile("w2_sc", [P, N], U8)
+        nc.vector.memset(x_sc[:].bitcast(I32), 0)
+        nc.gpsimd.memset(w2_sc[:].bitcast(I32), 0)
+
+        offs_sb = sb.tile([P, S // 16], U16, name="offs_sb")
+        nc.sync.dma_start(offs_sb[:], offs)
+        w1_raw = [tile(f"w1_raw{z}", [P, PACK, H], F32) for z in range(PASSES)]
+        for z in range(PASSES):
+            nc.sync.dma_start(
+                out=w1_raw[z][:], in_=w1[K_PASS * z : K_PASS * (z + 1), :].rearrange("(p j) c -> p j c", j=PACK)
+            )
+            if z == 0:
+                for q in range(4):
+                    nc.sync.dma_start(
+                        out=x_sc[32 * q : 32 * q + 4 * PASSES, :].bitcast(I32),
+                        in_=x_scales[:, 4 * q : 4 * q + 4, :].bitcast(I32),
+                    )
+        pos_sb = [sb.tile([P, V // 16], U16, name=f"pos_sb{d}") for d in range(D)]
+        nc.sync.dma_start(pos_sb[0][:], pos1)
+        nc.sync.dma_start(pos_sb[1][:], pos2)
+        x_wd = [tile(f"x_wd{z}", [P, T], I32) for z in range(PASSES)]
+        for z in range(PASSES):
+            nc.sync.dma_start(out=x_wd[z][:], in_=x_words[z].rearrange("p n t -> p (n t)").bitcast(I32))
+        w3_raw = [tile(f"w3_raw{s}", [P, PACK, H // 2], F32) for s in range(2)]
+        for s in range(2):
+            nc.sync.dma_start(
+                out=w3_raw[s][:], in_=w3[:, 256 * s : 256 * (s + 1)].rearrange("(p j) c -> p j c", j=PACK)
+            )
+        a_raw = [tile(f"a_raw{d}", [P, PACK, V], F32) for d in range(D)]
+        for d in range(D):
+            nc.sync.dma_start(
+                out=a_raw[d][:], in_=aT[:, V * d : V * (d + 1)].rearrange("(p j) c -> p j c", j=PACK)
+            )
+        w2_wd = tile("w2_wd", [P, N], I32)
+        nc.sync.dma_start(out=w2_wd[:], in_=w2_words[0].rearrange("p n t -> p (n t)").bitcast(I32))
+        for q in range(4):
+            nc.sync.dma_start(
+                out=w2_sc[32 * q : 32 * q + 4, :].bitcast(I32), in_=w2_scales[0, 4 * q : 4 * q + 4, :].bitcast(I32)
+            )
+
+        warm = tile("warm", [P, 2], F32)
+        nc.vector.memset(warm[:, 0:1], 0.0)
+        nc.scalar.activation(warm[:, 1:2], warm[:, 0:1], SILU)
+
+        xs = tile("xs", [P, S], U8)
+        xw = [tile(f"xw{z}", [P, S], U32) for z in range(PASSES)]
+        w1_q = {}
+        for z in range(PASSES):
+            src = w1_raw[z][:].rearrange("p j (m t) -> p m j t", t=PACK)
+            grouped = [tile(f"w1_g{z}{u}", [P, 2, P, PACK], BF16) for u in range(2)]
+            nc.scalar.copy(grouped[1][:].rearrange("p t m j -> p m j t"), src[:, :, :, 2:4])
+            nc.vector.tensor_copy(grouped[0][:].rearrange("p t m j -> p m j t"), src[:, :, :, 0:2])
+            if z == 0:
+                nc.vector.tensor_copy(xs[:], x_sc[:].indirect(offs_sb[:]))
+            for u in range(2):
+                w1_q[z, u] = quantise(f"w1_q{z}{u}", grouped[u][:].rearrange("p t m j -> p (t m j)"))
+
+        h_ps = [psum.tile([P, S], F32, name=f"h_ps{t}", tag=f"bank{t}") for t in range(1, PACK)]
+        h0_ps = [psum.tile([P, S // 2], F32, name=f"h0_ps{e}", tag=f"bank{7 * e}") for e in range(2)]
+        halves = [slice(0, S // 2), slice(S // 2, S)]
+
+        def layer(z, t, acc, cols):
+            codes, scales = w1_q[z, t // 2]
+            w_cols = slice(P * (t % 2), P * (t % 2 + 1))
+            nc.tensor.matmul_mx(
+                out=acc[:],
+                lhsT=codes[:, w_cols].bitcast(FP8X4),
+                lhsT_scale=scales[:, w_cols],
+                rhs=xw[z][:, cols].bitcast(FP8X4),
+                rhs_scale=xs[4 * z : P, cols],
+                start=(z == 0),
+                stop=(z == PASSES - 1),
+            )
+
+        for z in range(PASSES):
+            if z == 0:
+                nc.vector.tensor_copy(xw[z][:], x_wd[z][:].bitcast(U32).indirect(offs_sb[:]))
+            for e in range(2):
+                if z == 1:
+                    nc.vector.tensor_copy(
+                        xw[z][:, halves[e]], x_wd[z][:].bitcast(U32).indirect(offs_sb[:, 16 * e : 16 * (e + 1)])
+                    )
+                layer(z, 0, h0_ps[e], halves[e])
+            for t in range(1, PACK):
+                layer(z, t, h_ps[t - 1], slice(0, S))
+
+        w3_codes = tile("w3_codes", [P, H], U32)
+        w3_scales = tile("w3_scales", [P, H], U8)
+        w3_q = (w3_codes, w3_scales)
+
+        def w3_cast(s, copy, tag):
+            w3_g = tile(f"w3_g{s}", [P, PACK, 64, PACK], BF16, tag=tag)
+            copy(w3_g[:].rearrange("p t m j -> p m j t"), w3_raw[s][:].rearrange("p j (m t) -> p m j t", t=PACK))
+            return w3_g
+
+        def w3_quant(s, w3_g):
+            for t in range(PACK):
+                cols = slice(P * t + 64 * s, P * t + 64 * (s + 1))
+                nc.vector.quantize_mx(
+                    out=w3_codes[:, cols].bitcast(FP8X4),
+                    scales=w3_scales[:, cols],
+                    in_=w3_g[:, t].rearrange("p m j -> p (m j)"),
+                )
+
+        w3_quant(0, w3_cast(0, nc.vector.tensor_copy, "x_wd1"))
+
+        h = [tile(f"h{t}", [P, S], F32) for t in range(PACK)]
+        for e in range(2):
+            nc.scalar.activation(h[0][:, halves[e]], h0_ps[e][:], SILU)
+        for t in range(1, PACK):
+            nc.scalar.activation(h[t][:], h_ps[t - 1][:], SILU)
+        w3_g1 = w3_cast(1, nc.scalar.copy, "w1_q11_codes")
+        a_tags = ["w3_raw1", "w1_q11_scales"]
+        a_g = [tile(f"a_g{d}", [P, V, PACK], BF16, tag=a_tags[d]) for d in range(D)]
+        for d in range(D):
+            nc.scalar.copy(
+                a_g[d][:].rearrange("p (c i) j -> p c j i", i=4), a_raw[d][:].rearrange("p j (c i) -> p c j i", i=4)
+            )
+
+        g = {}
+
+        def gather(d, t):
+            if t % 2 == 0:
+                g[d, t // 2] = tile(f"g{d}{t // 2}", [P, 2, V], F32, tag=a_tags[0] if (d, t) == (0, 2) else None)
+            nc.vector.tensor_copy(g[d, t // 2][:, t % 2, :], h[t][:].indirect(pos_sb[d][:]))
+
+        f_ps = {}
+
+        def filters(d, w3_q):
+            a_codes, a_scales = quantise(f"a_q{d}", a_g[d][:].rearrange("p c j -> p (c j)"))
+            for t in range(PACK):
+                if t % 2 == 0:
+                    f_ps[d, t // 2] = psum.tile([P, 2, V], F32, name=f"f_ps{d}{t // 2}", tag=f"bank{4 + 2 * d + t // 2}")
+                cols = slice(P * t, P * (t + 1))
+                nc.tensor.matmul_mx(
+                    out=f_ps[d, t // 2][:, t % 2, :],
+                    lhsT=w3_q[0][:, cols].bitcast(FP8X4),
+                    lhsT_scale=w3_q[1][:, cols],
+                    rhs=a_codes[:].bitcast(FP8X4),
+                    rhs_scale=a_scales[:],
+                    start=True,
+                    stop=True,
+                )
+
+        prod = {}
+
+        def multiply(d):
+            prod[d] = tile(f"prod{d}", [P, PACK, V], F32, tag=a_tags[1] if d == 0 else None)
+            for u in range(2):
+                nc.vector.tensor_tensor(prod[d][:, 2 * u : 2 * u + 2, :], f_ps[d, u][:], g[d, u][:], MULT)
+
+        for t in range(2):
+            gather(0, t)
+            gather(1, t)
+        gather(1, 2)
+        w3_quant(1, w3_g1)
+        gather(1, 3)
+        filters(0, w3_q)
+        gather(0, 2)
+        gather(0, 3)
+        filters(1, w3_q)
+        multiply(0)
+        multiply(1)
+
+        z_g = [tile(f"z_g{s}", [P, P, PACK], BF16) for s in range(2)]
+        for s in range(2):
+            cols = slice(P * s, P * (s + 1))
+            nc.vector.tensor_tensor(
+                z_g[s][:].rearrange("p (c i) t -> p c t i", i=4),
+                prod[0][:, :, cols].rearrange("p t (c i) -> p c t i", i=4),
+                prod[1][:, :, cols].rearrange("p t (c i) -> p c t i", i=4),
+                ADD,
+            )
+        for s in range(2):
+            z_codes, z_scales = quantise(f"z_q{s}", z_g[s][:].rearrange("p v t -> p (v t)"))
+            o_ps = psum.tile([P, P], F32, name=f"o_ps{s}", tag=f"bank{s}")
+            nc.tensor.matmul_mx(
+                out=o_ps[:],
+                lhsT=w2_wd[:].bitcast(FP8X4),
+                lhsT_scale=w2_sc[:],
+                rhs=z_codes[:].bitcast(FP8X4),
+                rhs_scale=z_scales[:],
+                start=True,
+                stop=True,
+            )
+            o_sb = tile(f"o_sb{s}", [P, P], F32)
+            nc.scalar.activation(o_sb[:], o_ps[:], SILU)
+            nc.sync.dma_start(out=out[:, P * s : P * (s + 1)], in_=o_sb[:])

@@ -47,34 +47,29 @@ def tile_picked_dime_silu_p_kernel(
         nc.gpsimd.memset(w2_sc[:].bitcast(I32), 0)
 
         offs_sb = sb.tile([P, S // 16], U16, name="offs_sb")
-        nc.sync.dma_start(offs_sb[:], offs)
-        w1_raw = [tile(f"w1_raw{z}", [P, PACK, H], F32) for z in range(PASSES)]
-        for z in range(PASSES):
-            nc.sync.dma_start(
-                out=w1_raw[z][:], in_=w1[K_PASS * z : K_PASS * (z + 1), :].rearrange("(p j) c -> p j c", j=PACK)
-            )
-            if z == 0:
-                for q in range(4):
-                    nc.sync.dma_start(
-                        out=x_sc[32 * q : 32 * q + 4 * PASSES, :].bitcast(I32),
-                        in_=x_scales[:, 4 * q : 4 * q + 4, :].bitcast(I32),
-                    )
         pos_sb = [sb.tile([P, V // 16], U16, name=f"pos_sb{d}") for d in range(D)]
+        w3_raw = tile("w3_raw", [P, PACK, H], F32)
+        a_raw = [tile(f"a_raw{d}", [P, PACK, V], F32) for d in range(D)]
+        w1_raw = [tile(f"w1_raw{z}", [P, PACK, H], F32) for z in range(PASSES)]
+        x_wd = [tile(f"x_wd{z}", [P, T], I32) for z in range(PASSES)]
+
+        def load_rows(dst, src):
+            nc.sync.dma_start(out=dst[:], in_=src.rearrange("(p j) c -> p j c", j=PACK))
+
+        load_rows(w3_raw, w3)
+        for q in range(4):
+            nc.sync.dma_start(
+                out=x_sc[32 * q : 32 * q + 4 * PASSES, :].bitcast(I32),
+                in_=x_scales[:, 4 * q : 4 * q + 4, :].bitcast(I32),
+            )
+        nc.sync.dma_start(offs_sb[:], offs)
+        load_rows(a_raw[0], aT[:, 0:V])
+        for z in range(PASSES):
+            load_rows(w1_raw[z], w1[K_PASS * z : K_PASS * (z + 1), :])
+            nc.sync.dma_start(out=x_wd[z][:], in_=x_words[z].rearrange("p n t -> p (n t)").bitcast(I32))
+        load_rows(a_raw[1], aT[:, V : 2 * V])
         nc.sync.dma_start(pos_sb[0][:], pos1)
         nc.sync.dma_start(pos_sb[1][:], pos2)
-        x_wd = [tile(f"x_wd{z}", [P, T], I32) for z in range(PASSES)]
-        for z in range(PASSES):
-            nc.sync.dma_start(out=x_wd[z][:], in_=x_words[z].rearrange("p n t -> p (n t)").bitcast(I32))
-        w3_raw = [tile(f"w3_raw{s}", [P, PACK, H // 2], F32) for s in range(2)]
-        for s in range(2):
-            nc.sync.dma_start(
-                out=w3_raw[s][:], in_=w3[:, 256 * s : 256 * (s + 1)].rearrange("(p j) c -> p j c", j=PACK)
-            )
-        a_raw = [tile(f"a_raw{d}", [P, PACK, V], F32) for d in range(D)]
-        for d in range(D):
-            nc.sync.dma_start(
-                out=a_raw[d][:], in_=aT[:, V * d : V * (d + 1)].rearrange("(p j) c -> p j c", j=PACK)
-            )
         w2_wd = tile("w2_wd", [P, N], I32)
         nc.sync.dma_start(out=w2_wd[:], in_=w2_words[0].rearrange("p n t -> p (n t)").bitcast(I32))
         for q in range(4):
@@ -88,16 +83,48 @@ def tile_picked_dime_silu_p_kernel(
 
         xs = tile("xs", [P, S], U8)
         xw = [tile(f"xw{z}", [P, S], U32) for z in range(PASSES)]
-        w1_q = {}
-        for z in range(PASSES):
-            src = w1_raw[z][:].rearrange("p j (m t) -> p m j t", t=PACK)
-            grouped = [tile(f"w1_g{z}{u}", [P, 2, P, PACK], BF16) for u in range(2)]
+
+        def weights(name, raw, tags=(None, None)):
+            src = raw[:].rearrange("p j (m t) -> p m j t", t=PACK)
+            grouped = [tile(f"{name}_g{u}", [P, 2, P, PACK], BF16, tag=tags[u]) for u in range(2)]
             nc.scalar.copy(grouped[1][:].rearrange("p t m j -> p m j t"), src[:, :, :, 2:4])
             nc.vector.tensor_copy(grouped[0][:].rearrange("p t m j -> p m j t"), src[:, :, :, 0:2])
-            if z == 0:
-                nc.vector.tensor_copy(xs[:], x_sc[:].indirect(offs_sb[:]))
+            return [quantise(f"{name}_q{u}", grouped[u][:].rearrange("p t m j -> p (t m j)")) for u in range(2)]
+
+        f_sb = [tile(f"f_sb{d}", [P, PACK, V], F32) for d in range(D)]
+
+        def filters(d, tag):
+            a_g = tile(f"a_g{d}", [P, V, PACK], BF16, tag=tag)
+            nc.vector.tensor_copy(
+                a_g[:].rearrange("p (c i) j -> p c j i", i=4), a_raw[d][:].rearrange("p j (c i) -> p c j i", i=4)
+            )
+            a_codes, a_scales = quantise(f"a_q{d}", a_g[:].rearrange("p c j -> p (c j)"))
+            banks = []
             for u in range(2):
-                w1_q[z, u] = quantise(f"w1_q{z}{u}", grouped[u][:].rearrange("p t m j -> p (t m j)"))
+                f_ps = psum.tile([P, 2, V], F32, name=f"f_ps{d}{u}", tag=f"bank{4 + u}")
+                codes, scales = w3_q[u]
+                for e in range(2):
+                    cols = slice(P * e, P * (e + 1))
+                    nc.tensor.matmul_mx(
+                        out=f_ps[:, e, :],
+                        lhsT=codes[:, cols].bitcast(FP8X4),
+                        lhsT_scale=scales[:, cols],
+                        rhs=a_codes[:].bitcast(FP8X4),
+                        rhs_scale=a_scales[:],
+                        start=True,
+                        stop=True,
+                    )
+                banks.append(f_ps)
+            return banks
+
+        def drain(d, banks):
+            for u in range(2):
+                nc.scalar.copy(f_sb[d][:, 2 * u : 2 * u + 2, :], banks[u][:])
+
+        w3_q = weights("w3", w3_raw)
+        nc.vector.tensor_copy(xs[:], x_sc[:].indirect(offs_sb[:]))
+        drain(0, filters(0, None))
+        w1_q = {}
 
         h_ps = [psum.tile([P, S], F32, name=f"h_ps{t}", tag=f"bank{t}") for t in range(1, PACK)]
         h0_ps = [psum.tile([P, S // 2], F32, name=f"h0_ps{e}", tag=f"bank{7 * e}") for e in range(2)]
@@ -117,6 +144,7 @@ def tile_picked_dime_silu_p_kernel(
             )
 
         for z in range(PASSES):
+            w1_q[z, 0], w1_q[z, 1] = weights(f"w1{z}", w1_raw[z])
             if z == 0:
                 nc.vector.tensor_copy(xw[z][:], x_wd[z][:].bitcast(U32).indirect(offs_sb[:]))
             for e in range(2):
@@ -128,83 +156,17 @@ def tile_picked_dime_silu_p_kernel(
             for t in range(1, PACK):
                 layer(z, t, h_ps[t - 1], slice(0, S))
 
-        w3_codes = tile("w3_codes", [P, H], U32)
-        w3_scales = tile("w3_scales", [P, H], U8)
-        w3_q = (w3_codes, w3_scales)
-
-        def w3_cast(s, copy, tag):
-            w3_g = tile(f"w3_g{s}", [P, PACK, 64, PACK], BF16, tag=tag)
-            copy(w3_g[:].rearrange("p t m j -> p m j t"), w3_raw[s][:].rearrange("p j (m t) -> p m j t", t=PACK))
-            return w3_g
-
-        def w3_quant(s, w3_g):
-            for t in range(PACK):
-                cols = slice(P * t + 64 * s, P * t + 64 * (s + 1))
-                nc.vector.quantize_mx(
-                    out=w3_codes[:, cols].bitcast(FP8X4),
-                    scales=w3_scales[:, cols],
-                    in_=w3_g[:, t].rearrange("p m j -> p (m j)"),
-                )
-
-        w3_quant(0, w3_cast(0, nc.vector.tensor_copy, "x_wd1"))
-
+        banks = filters(1, "x_wd1")
         h = [tile(f"h{t}", [P, S], F32) for t in range(PACK)]
         for e in range(2):
             nc.scalar.activation(h[0][:, halves[e]], h0_ps[e][:], SILU)
         for t in range(1, PACK):
             nc.scalar.activation(h[t][:], h_ps[t - 1][:], SILU)
-        w3_g1 = w3_cast(1, nc.scalar.copy, "w1_q11_codes")
-        a_tags = ["w3_raw1", "w1_q11_scales"]
-        a_g = [tile(f"a_g{d}", [P, V, PACK], BF16, tag=a_tags[d]) for d in range(D)]
+        drain(1, banks)
+        prod = [tile(f"prod{d}", [P, PACK, V], F32) for d in range(D)]
         for d in range(D):
-            nc.scalar.copy(
-                a_g[d][:].rearrange("p (c i) j -> p c j i", i=4), a_raw[d][:].rearrange("p j (c i) -> p c j i", i=4)
-            )
-
-        g = {}
-
-        def gather(d, t):
-            if t % 2 == 0:
-                g[d, t // 2] = tile(f"g{d}{t // 2}", [P, 2, V], F32, tag=a_tags[0] if (d, t) == (0, 2) else None)
-            nc.vector.tensor_copy(g[d, t // 2][:, t % 2, :], h[t][:].indirect(pos_sb[d][:]))
-
-        f_ps = {}
-
-        def filters(d, w3_q):
-            a_codes, a_scales = quantise(f"a_q{d}", a_g[d][:].rearrange("p c j -> p (c j)"))
             for t in range(PACK):
-                if t % 2 == 0:
-                    f_ps[d, t // 2] = psum.tile([P, 2, V], F32, name=f"f_ps{d}{t // 2}", tag=f"bank{4 + 2 * d + t // 2}")
-                cols = slice(P * t, P * (t + 1))
-                nc.tensor.matmul_mx(
-                    out=f_ps[d, t // 2][:, t % 2, :],
-                    lhsT=w3_q[0][:, cols].bitcast(FP8X4),
-                    lhsT_scale=w3_q[1][:, cols],
-                    rhs=a_codes[:].bitcast(FP8X4),
-                    rhs_scale=a_scales[:],
-                    start=True,
-                    stop=True,
-                )
-
-        prod = {}
-
-        def multiply(d):
-            prod[d] = tile(f"prod{d}", [P, PACK, V], F32, tag=a_tags[1] if d == 0 else None)
-            for u in range(2):
-                nc.vector.tensor_tensor(prod[d][:, 2 * u : 2 * u + 2, :], f_ps[d, u][:], g[d, u][:], MULT)
-
-        for t in range(2):
-            gather(0, t)
-            gather(1, t)
-        gather(1, 2)
-        w3_quant(1, w3_g1)
-        gather(1, 3)
-        filters(0, w3_q)
-        gather(0, 2)
-        gather(0, 3)
-        filters(1, w3_q)
-        multiply(0)
-        multiply(1)
+                nc.vector.tensor_tensor(prod[d][:, t, :], h[t][:].indirect(pos_sb[d][:]), f_sb[d][:, t, :], MULT)
 
         z_g = [tile(f"z_g{s}", [P, P, PACK], BF16) for s in range(2)]
         for s in range(2):

@@ -3,7 +3,8 @@ from contextlib import ExitStack
 import concourse.mybir as mybir
 
 K, T, S, V, H, N, J = 1024, 2048, 512, 256, 512, 128, 512
-FLOPS = 2 * K * H * S + 2 * J * H * 2 * V + 2 * H * N * V
+D = 2
+FLOPS = 2 * K * H * S + 2 * J * H * D * V + 2 * H * N * V
 
 F32 = mybir.dt.float32
 BF16 = mybir.dt.bfloat16
@@ -20,7 +21,9 @@ P = 128
 PACK = 4
 K_PASS = P * PACK
 PASSES = K // K_PASS
-D = 2
+QUADRANTS = 4
+PER_COLUMN = 16
+RUN = 4
 
 
 def tile_picked_dime_silu_p_kernel(
@@ -46,8 +49,8 @@ def tile_picked_dime_silu_p_kernel(
         nc.vector.memset(x_sc[:].bitcast(I32), 0)
         nc.gpsimd.memset(w2_sc[:].bitcast(I32), 0)
 
-        offs_sb = sb.tile([P, S // 16], U16, name="offs_sb")
-        pos_sb = [sb.tile([P, V // 16], U16, name=f"pos_sb{d}") for d in range(D)]
+        offs_sb = sb.tile([P, S // PER_COLUMN], U16, name="offs_sb")
+        pos_sb = [sb.tile([P, V // PER_COLUMN], U16, name=f"pos_sb{d}") for d in range(D)]
         w3_raw = tile("w3_raw", [P, PACK, H], F32)
         a_raw = [tile(f"a_raw{d}", [P, PACK, V], F32) for d in range(D)]
         w1_raw = [tile(f"w1_raw{z}", [P, PACK, H], F32) for z in range(PASSES)]
@@ -57,7 +60,7 @@ def tile_picked_dime_silu_p_kernel(
             nc.sync.dma_start(out=dst[:], in_=src.rearrange("(p j) c -> p j c", j=PACK))
 
         load_rows(w3_raw, w3)
-        for q in range(4):
+        for q in range(QUADRANTS):
             nc.sync.dma_start(
                 out=x_sc[32 * q : 32 * q + 4 * PASSES, :].bitcast(I32),
                 in_=x_scales[:, 4 * q : 4 * q + 4, :].bitcast(I32),
@@ -72,23 +75,22 @@ def tile_picked_dime_silu_p_kernel(
         nc.sync.dma_start(pos_sb[1][:], pos2)
         w2_wd = tile("w2_wd", [P, N], I32)
         nc.sync.dma_start(out=w2_wd[:], in_=w2_words[0].rearrange("p n t -> p (n t)").bitcast(I32))
-        for q in range(4):
+        for q in range(QUADRANTS):
             nc.sync.dma_start(
                 out=w2_sc[32 * q : 32 * q + 4, :].bitcast(I32), in_=w2_scales[0, 4 * q : 4 * q + 4, :].bitcast(I32)
             )
 
-        warm = tile("warm", [P, 2], F32)
-        nc.vector.memset(warm[:, 0:1], 0.0)
-        nc.scalar.activation(warm[:, 1:2], warm[:, 0:1], SILU)
-
         xs = tile("xs", [P, S], U8)
         xw = [tile(f"xw{z}", [P, S], U32) for z in range(PASSES)]
 
-        def weights(name, raw, tags=(None, None)):
+        def weights(name, raw, scalar_m):
             src = raw[:].rearrange("p j (m t) -> p m j t", t=PACK)
-            grouped = [tile(f"{name}_g{u}", [P, 2, P, PACK], BF16, tag=tags[u]) for u in range(2)]
-            nc.scalar.copy(grouped[1][:].rearrange("p t m j -> p m j t"), src[:, :, :, 2:4])
-            nc.vector.tensor_copy(grouped[0][:].rearrange("p t m j -> p m j t"), src[:, :, :, 0:2])
+            grouped = [tile(f"{name}_g{u}", [P, 2, P, PACK], BF16) for u in range(2)]
+            dst = [g[:].rearrange("p t m j -> p m j t") for g in grouped]
+            nc.scalar.copy(dst[1][:, 0:scalar_m], src[:, 0:scalar_m, :, 2:4])
+            nc.vector.tensor_copy(dst[0], src[:, :, :, 0:2])
+            if scalar_m < P:
+                nc.vector.tensor_copy(dst[1][:, scalar_m:P], src[:, scalar_m:P, :, 2:4])
             return [quantise(f"{name}_q{u}", grouped[u][:].rearrange("p t m j -> p (t m j)")) for u in range(2)]
 
         f_sb = [tile(f"f_sb{d}", [P, PACK, V], F32) for d in range(D)]
@@ -96,17 +98,17 @@ def tile_picked_dime_silu_p_kernel(
         def filters(d, tag):
             a_g = tile(f"a_g{d}", [P, V, PACK], BF16, tag=tag)
             nc.vector.tensor_copy(
-                a_g[:].rearrange("p (c i) j -> p c j i", i=4), a_raw[d][:].rearrange("p j (c i) -> p c j i", i=4)
+                a_g[:].rearrange("p (c i) j -> p c j i", i=RUN), a_raw[d][:].rearrange("p j (c i) -> p c j i", i=RUN)
             )
             a_codes, a_scales = quantise(f"a_q{d}", a_g[:].rearrange("p c j -> p (c j)"))
-            banks = []
+            f_ps = []
             for u in range(2):
-                f_ps = psum.tile([P, 2, V], F32, name=f"f_ps{d}{u}", tag=f"bank{4 + u}")
+                bank = psum.tile([P, 2, V], F32, name=f"f_ps{d}{u}", tag=f"bank{PACK + u}")
                 codes, scales = w3_q[u]
                 for e in range(2):
                     cols = slice(P * e, P * (e + 1))
                     nc.tensor.matmul_mx(
-                        out=f_ps[:, e, :],
+                        out=bank[:, e, :],
                         lhsT=codes[:, cols].bitcast(FP8X4),
                         lhsT_scale=scales[:, cols],
                         rhs=a_codes[:].bitcast(FP8X4),
@@ -114,24 +116,25 @@ def tile_picked_dime_silu_p_kernel(
                         start=True,
                         stop=True,
                     )
-                banks.append(f_ps)
-            return banks
+                f_ps.append(bank)
+            return f_ps
 
-        def drain(d, banks):
+        def drain(d, f_ps):
             for u in range(2):
-                nc.scalar.copy(f_sb[d][:, 2 * u : 2 * u + 2, :], banks[u][:])
+                nc.scalar.copy(f_sb[d][:, 2 * u : 2 * u + 2, :], f_ps[u][:])
 
-        w3_q = weights("w3", w3_raw)
+        w3_q = weights("w3", w3_raw, P)
         nc.vector.tensor_copy(xs[:], x_sc[:].indirect(offs_sb[:]))
         drain(0, filters(0, None))
-        w1_q = {}
 
         h_ps = [psum.tile([P, S], F32, name=f"h_ps{t}", tag=f"bank{t}") for t in range(1, PACK)]
         h0_ps = [psum.tile([P, S // 2], F32, name=f"h0_ps{e}", tag=f"bank{7 * e}") for e in range(2)]
         halves = [slice(0, S // 2), slice(S // 2, S)]
+        half_columns = S // 2 // PER_COLUMN
+        w1_q = {}
 
         def layer(z, t, acc, cols):
-            codes, scales = w1_q[z, t // 2]
+            codes, scales = w1_q[z][t // 2]
             w_cols = slice(P * (t % 2), P * (t % 2 + 1))
             nc.tensor.matmul_mx(
                 out=acc[:],
@@ -144,37 +147,44 @@ def tile_picked_dime_silu_p_kernel(
             )
 
         for z in range(PASSES):
-            w1_q[z, 0], w1_q[z, 1] = weights(f"w1{z}", w1_raw[z])
-            if z == 0:
-                nc.vector.tensor_copy(xw[z][:], x_wd[z][:].bitcast(U32).indirect(offs_sb[:]))
+            last = z == PASSES - 1
+            w1_q[z] = weights(f"w1{z}", w1_raw[z], P // 2 if last else P)
+            window = x_wd[z][:].bitcast(U32)
+            if not last:
+                nc.vector.tensor_copy(xw[z][:], window.indirect(offs_sb[:]))
             for e in range(2):
-                if z == 1:
-                    nc.vector.tensor_copy(
-                        xw[z][:, halves[e]], x_wd[z][:].bitcast(U32).indirect(offs_sb[:, 16 * e : 16 * (e + 1)])
-                    )
+                if last:
+                    entries = offs_sb[:, half_columns * e : half_columns * (e + 1)]
+                    nc.vector.tensor_copy(xw[z][:, halves[e]], window.indirect(entries))
                 layer(z, 0, h0_ps[e], halves[e])
             for t in range(1, PACK):
                 layer(z, t, h_ps[t - 1], slice(0, S))
 
-        banks = filters(1, "x_wd1")
+        f1_ps = filters(1, f"x_wd{PASSES - 1}")
         h = [tile(f"h{t}", [P, S], F32) for t in range(PACK)]
         for e in range(2):
             nc.scalar.activation(h[0][:, halves[e]], h0_ps[e][:], SILU)
         for t in range(1, PACK):
             nc.scalar.activation(h[t][:], h_ps[t - 1][:], SILU)
-        drain(1, banks)
+        drain(1, f1_ps)
+
         prod = [tile(f"prod{d}", [P, PACK, V], F32) for d in range(D)]
         for d in range(D):
             for t in range(PACK):
-                nc.vector.tensor_tensor(prod[d][:, t, :], h[t][:].indirect(pos_sb[d][:]), f_sb[d][:, t, :], MULT)
+                pieces = 2 if (d, t) == (D - 1, PACK - 1) else 1
+                n = V // pieces
+                for s in range(pieces):
+                    cols = slice(n * s, n * (s + 1))
+                    entries = pos_sb[d][:, cols.start // PER_COLUMN : cols.stop // PER_COLUMN]
+                    nc.vector.tensor_tensor(prod[d][:, t, cols], h[t][:].indirect(entries), f_sb[d][:, t, cols], MULT)
 
         z_g = [tile(f"z_g{s}", [P, P, PACK], BF16) for s in range(2)]
         for s in range(2):
             cols = slice(P * s, P * (s + 1))
             nc.vector.tensor_tensor(
-                z_g[s][:].rearrange("p (c i) t -> p c t i", i=4),
-                prod[0][:, :, cols].rearrange("p t (c i) -> p c t i", i=4),
-                prod[1][:, :, cols].rearrange("p t (c i) -> p c t i", i=4),
+                z_g[s][:].rearrange("p (c i) t -> p c t i", i=RUN),
+                prod[0][:, :, cols].rearrange("p t (c i) -> p c t i", i=RUN),
+                prod[1][:, :, cols].rearrange("p t (c i) -> p c t i", i=RUN),
                 ADD,
             )
         for s in range(2):

@@ -59,17 +59,34 @@ def tile_picked_dime_silu_p_kernel(
         def load_rows(dst, src):
             nc.sync.dma_start(out=dst[:], in_=src.rearrange("(p j) c -> p j c", j=PACK))
 
-        load_rows(w3_raw, w3)
-        for q in range(QUADRANTS):
-            nc.sync.dma_start(
-                out=x_sc[32 * q : 32 * q + 4 * PASSES, :].bitcast(I32),
-                in_=x_scales[:, 4 * q : 4 * q + 4, :].bitcast(I32),
-            )
-        nc.sync.dma_start(offs_sb[:], offs)
-        load_rows(a_raw[0], aT[:, 0:V])
-        for z in range(PASSES):
-            load_rows(w1_raw[z], w1[K_PASS * z : K_PASS * (z + 1), :])
+        def load_words(z):
             nc.sync.dma_start(out=x_wd[z][:], in_=x_words[z].rearrange("p n t -> p (n t)").bitcast(I32))
+
+        xs_rows = tile("xs_rows", [P, S], U8)
+        xs = [tile(f"xs{z}", [P, S], U8) for z in range(PASSES)]
+        for z in range(PASSES):
+            nc.gpsimd.memset(xs[z][:].bitcast(I32), 0)
+
+        def place_scales(first, last):
+            for g in range(first, last):
+                z, q = divmod(g, QUADRANTS)
+                nc.sync.dma_start(
+                    out=xs[z][32 * q : 32 * q + 4, :].bitcast(I32),
+                    in_=xs_rows[16 * g : 16 * (g + 1) : 4, :].bitcast(I32),
+                )
+
+        load_rows(a_raw[0], aT[:, 0:V])
+        nc.sync.dma_start(out=x_sc[0:P:4, :].bitcast(I32), in_=x_scales.rearrange("z r n -> (z r) n").bitcast(I32))
+        nc.sync.dma_start(offs_sb[:], offs)
+        nc.vector.tensor_copy(xs_rows[:], x_sc[:].indirect(offs_sb[:]))
+        load_rows(w3_raw, w3)
+        load_rows(w1_raw[0], w1[0:K_PASS, :])
+        place_scales(0, 3)
+        load_words(0)
+        place_scales(3, 6)
+        load_rows(w1_raw[1], w1[K_PASS : 2 * K_PASS, :])
+        place_scales(6, 8)
+        load_words(1)
         load_rows(a_raw[1], aT[:, V : 2 * V])
         nc.sync.dma_start(pos_sb[0][:], pos1)
         nc.sync.dma_start(pos_sb[1][:], pos2)
@@ -80,7 +97,6 @@ def tile_picked_dime_silu_p_kernel(
                 out=w2_sc[32 * q : 32 * q + 4, :].bitcast(I32), in_=w2_scales[0, 4 * q : 4 * q + 4, :].bitcast(I32)
             )
 
-        xs = tile("xs", [P, S], U8)
         xw = [tile(f"xw{z}", [P, S], U32) for z in range(PASSES)]
 
         def weights(name, raw, scalar_m):
@@ -124,7 +140,6 @@ def tile_picked_dime_silu_p_kernel(
                 nc.scalar.copy(f_sb[d][:, 2 * u : 2 * u + 2, :], f_ps[u][:])
 
         w3_q = weights("w3", w3_raw, P)
-        nc.vector.tensor_copy(xs[:], x_sc[:].indirect(offs_sb[:]))
         drain(0, filters(0, None))
 
         h_ps = [psum.tile([P, S], F32, name=f"h_ps{t}", tag=f"bank{t}") for t in range(1, PACK)]
@@ -141,7 +156,7 @@ def tile_picked_dime_silu_p_kernel(
                 lhsT=codes[:, w_cols].bitcast(FP8X4),
                 lhsT_scale=scales[:, w_cols],
                 rhs=xw[z][:, cols].bitcast(FP8X4),
-                rhs_scale=xs[4 * z : P, cols],
+                rhs_scale=xs[z][:, cols],
                 start=(z == 0),
                 stop=(z == PASSES - 1),
             )
@@ -168,7 +183,7 @@ def tile_picked_dime_silu_p_kernel(
             nc.scalar.activation(h[t][:], h_ps[t - 1][:], SILU)
         drain(1, f1_ps)
 
-        prod = [tile(f"prod{d}", [P, PACK, V], F32) for d in range(D)]
+        prod = [tile(f"prod{d}", [P, PACK, V], F32, tag=None if d else f"x_wd{PASSES - 1}") for d in range(D)]
         for d in range(D):
             for t in range(PACK):
                 pieces = 2 if (d, t) == (D - 1, PACK - 1) else 1

@@ -63,15 +63,14 @@ def tile_picked_dime_silu_p_kernel(
             nc.sync.dma_start(out=x_wd[z][:], in_=x_words[z].rearrange("p n t -> p (n t)").bitcast(I32))
 
         xs_rows = tile("xs_rows", [P, S], U8)
-        xs = [tile(f"xs{z}", [P, S], U8) for z in range(PASSES)]
-        for z in range(PASSES):
-            nc.gpsimd.memset(xs[z][:].bitcast(I32), 0)
+        xs = tile("xs", [P, S], U8)
+        nc.gpsimd.memset(xs[:].bitcast(I32), 0)
 
         def place_scales(first, last):
             for g in range(first, last):
                 z, q = divmod(g, QUADRANTS)
                 nc.sync.dma_start(
-                    out=xs[z][32 * q : 32 * q + 4, :].bitcast(I32),
+                    out=xs[32 * q + 4 * z : 32 * q + 4 * z + 4, :].bitcast(I32),
                     in_=xs_rows[16 * g : 16 * (g + 1) : 4, :].bitcast(I32),
                 )
 
@@ -113,10 +112,21 @@ def tile_picked_dime_silu_p_kernel(
 
         def filters(d, tag):
             a_g = tile(f"a_g{d}", [P, V, PACK], BF16, tag=tag)
-            nc.vector.tensor_copy(
-                a_g[:].rearrange("p (c i) j -> p c j i", i=RUN), a_raw[d][:].rearrange("p j (c i) -> p c j i", i=RUN)
-            )
-            a_codes, a_scales = quantise(f"a_q{d}", a_g[:].rearrange("p c j -> p (c j)"))
+            a_codes = tile(f"a_codes{d}", [P, V], U32)
+            a_scales = tile(f"a_scales{d}", [P, V], U8)
+            for e in range(2):
+                cols = slice(P * e, P * (e + 1))
+                nc.vector.tensor_copy(
+                    a_g[:, cols, :].rearrange("p (c i) j -> p c j i", i=RUN),
+                    a_raw[d][:, :, cols].rearrange("p j (c i) -> p c j i", i=RUN),
+                )
+            for e in range(2):
+                cols = slice(P * e, P * (e + 1))
+                nc.vector.quantize_mx(
+                    out=a_codes[:, cols].bitcast(FP8X4),
+                    scales=a_scales[:, cols],
+                    in_=a_g[:, cols, :].rearrange("p c j -> p (c j)"),
+                )
             f_ps = []
             for u in range(2):
                 bank = psum.tile([P, 2, V], F32, name=f"f_ps{d}{u}", tag=f"bank{PACK + u}")
@@ -156,7 +166,7 @@ def tile_picked_dime_silu_p_kernel(
                 lhsT=codes[:, w_cols].bitcast(FP8X4),
                 lhsT_scale=scales[:, w_cols],
                 rhs=xw[z][:, cols].bitcast(FP8X4),
-                rhs_scale=xs[z][:, cols],
+                rhs_scale=xs[4 * z : P, cols],
                 start=(z == 0),
                 stop=(z == PASSES - 1),
             )

@@ -63,28 +63,26 @@ def tile_picked_dime_silu_p_kernel(
             nc.sync.dma_start(out=x_wd[z][:], in_=x_words[z].rearrange("p n t -> p (n t)").bitcast(I32))
 
         xs_rows = tile("xs_rows", [P, S], U8)
-        xs = tile("xs", [P, S], U8)
+        xs = tile("xs", [P, PASSES * S], U8)
         nc.gpsimd.memset(xs[:].bitcast(I32), 0)
 
         def place_scales(first, last):
-            for g in range(first, last):
-                z, q = divmod(g, QUADRANTS)
+            for q in range(first, last):
                 nc.sync.dma_start(
-                    out=xs[32 * q + 4 * z : 32 * q + 4 * z + 4, :].bitcast(I32),
-                    in_=xs_rows[16 * g : 16 * (g + 1) : 4, :].bitcast(I32),
+                    out=xs[32 * q : 32 * q + 4, :].bitcast(I32).rearrange("r (z n) -> r z n", z=PASSES),
+                    in_=xs_rows[32 * q : 32 * (q + 1) : 4, :].bitcast(I32),
                 )
 
         load_rows(a_raw[0], aT[:, 0:V])
-        nc.sync.dma_start(out=x_sc[0:P:4, :].bitcast(I32), in_=x_scales.rearrange("z r n -> (z r) n").bitcast(I32))
+        nc.sync.dma_start(out=x_sc[0:P:4, :].bitcast(I32), in_=x_scales.bitcast(I32).rearrange("z r n -> r z n"))
         nc.sync.dma_start(offs_sb[:], offs)
         nc.vector.tensor_copy(xs_rows[:], x_sc[:].indirect(offs_sb[:]))
         load_rows(w3_raw, w3)
         load_rows(w1_raw[0], w1[0:K_PASS, :])
-        place_scales(0, 3)
         load_words(0)
-        place_scales(3, 6)
+        place_scales(0, QUADRANTS - 1)
         load_rows(w1_raw[1], w1[K_PASS : 2 * K_PASS, :])
-        place_scales(6, 8)
+        place_scales(QUADRANTS - 1, QUADRANTS)
         load_words(1)
         load_rows(a_raw[1], aT[:, V : 2 * V])
         nc.sync.dma_start(pos_sb[0][:], pos1)
@@ -166,7 +164,7 @@ def tile_picked_dime_silu_p_kernel(
                 lhsT=codes[:, w_cols].bitcast(FP8X4),
                 lhsT_scale=scales[:, w_cols],
                 rhs=xw[z][:, cols].bitcast(FP8X4),
-                rhs_scale=xs[4 * z : P, cols],
+                rhs_scale=xs[:, S * z + cols.start : S * z + cols.stop],
                 start=(z == 0),
                 stop=(z == PASSES - 1),
             )

@@ -49,6 +49,10 @@ def tile_picked_dime_silu_p_kernel(
         nc.vector.memset(x_sc[:].bitcast(I32), 0)
         nc.gpsimd.memset(w2_sc[:].bitcast(I32), 0)
 
+        warm = tile("warm", [P, 16], F32)
+        nc.gpsimd.memset(warm[:, 0:1], 0.0)
+        nc.scalar.activation(warm[:, 8:9], warm[:, 0:1], SILU)
+
         offs_sb = sb.tile([P, S // PER_COLUMN], U16, name="offs_sb")
         pos_sb = [sb.tile([P, V // PER_COLUMN], U16, name=f"pos_sb{d}") for d in range(D)]
         w3_raw = tile("w3_raw", [P, PACK, H], F32)
@@ -151,7 +155,11 @@ def tile_picked_dime_silu_p_kernel(
         drain(0, filters(0, None))
 
         h_ps = [psum.tile([P, S], F32, name=f"h_ps{t}", tag=f"bank{t}") for t in range(1, PACK)]
-        h0_ps = [psum.tile([P, S // 2], F32, name=f"h0_ps{e}", tag=f"bank{7 * e}") for e in range(2)]
+        h0_cols = [slice(0, S // 2), slice(S // 2, 3 * S // 4), slice(3 * S // 4, S)]
+        h0_ps = [
+            psum.tile([P, cols.stop - cols.start], F32, name=f"h0_ps{e}", tag=f"bank{(0, 6, 7)[e]}")
+            for e, cols in enumerate(h0_cols)
+        ]
         halves = [slice(0, S // 2), slice(S // 2, S)]
         half_columns = S // 2 // PER_COLUMN
         w1_q = {}
@@ -171,27 +179,27 @@ def tile_picked_dime_silu_p_kernel(
 
         for z in range(PASSES):
             last = z == PASSES - 1
-            w1_q[z] = weights(f"w1{z}", w1_raw[z], P // 2 if last else P)
+            w1_q[z] = weights(f"w1{z}", w1_raw[z], P)
             window = x_wd[z][:].bitcast(U32)
             if not last:
                 nc.vector.tensor_copy(xw[z][:], window.indirect(offs_sb[:]))
-            for e in range(2):
-                if last:
+            for e, cols in enumerate(h0_cols):
+                if last and e < 2:
                     entries = offs_sb[:, half_columns * e : half_columns * (e + 1)]
                     nc.vector.tensor_copy(xw[z][:, halves[e]], window.indirect(entries))
-                layer(z, 0, h0_ps[e], halves[e])
+                layer(z, 0, h0_ps[e], cols)
             for t in range(1, PACK):
                 layer(z, t, h_ps[t - 1], slice(0, S))
 
-        f1_ps = filters(1, f"x_wd{PASSES - 1}")
+        f1_ps = filters(1, None)
         h = [tile(f"h{t}", [P, S], F32) for t in range(PACK)]
-        for e in range(2):
-            nc.scalar.activation(h[0][:, halves[e]], h0_ps[e][:], SILU)
+        for e, cols in enumerate(h0_cols):
+            nc.scalar.activation(h[0][:, cols], h0_ps[e][:], SILU)
         for t in range(1, PACK):
             nc.scalar.activation(h[t][:], h_ps[t - 1][:], SILU)
         drain(1, f1_ps)
 
-        prod = [tile(f"prod{d}", [P, PACK, V], F32, tag=None if d else f"x_wd{PASSES - 1}") for d in range(D)]
+        prod = [tile(f"prod{d}", [P, PACK, V], F32, tag=None if d else "a_raw1") for d in range(D)]
         for d in range(D):
             for t in range(PACK):
                 pieces = 2 if (d, t) == (D - 1, PACK - 1) else 1

@@ -49,10 +49,6 @@ def tile_picked_dime_silu_p_kernel(
         nc.vector.memset(x_sc[:].bitcast(I32), 0)
         nc.gpsimd.memset(w2_sc[:].bitcast(I32), 0)
 
-        warm = tile("warm", [P, 16], F32)
-        nc.gpsimd.memset(warm[:, 0:1], 0.0)
-        nc.scalar.activation(warm[:, 8:9], warm[:, 0:1], SILU)
-
         offs_sb = sb.tile([P, S // PER_COLUMN], U16, name="offs_sb")
         pos_sb = [sb.tile([P, V // PER_COLUMN], U16, name=f"pos_sb{d}") for d in range(D)]
         w3_raw = tile("w3_raw", [P, PACK, H], F32)

@@ -1,6 +1,7 @@
 from contextlib import ExitStack
 
 import concourse.mybir as mybir
+from concourse.masks import make_identity
 
 K, T, S, V, H, N, J = 1024, 2048, 512, 256, 512, 128, 512
 D = 2
@@ -48,6 +49,8 @@ def tile_picked_dime_silu_p_kernel(
         w2_sc = tile("w2_sc", [P, N], U8)
         nc.vector.memset(x_sc[:].bitcast(I32), 0)
         nc.gpsimd.memset(w2_sc[:].bitcast(I32), 0)
+        ident = tile("ident", [P, P], F32)
+        make_identity(nc, ident[:])
 
         offs_sb = sb.tile([P, S // PER_COLUMN], U16, name="offs_sb")
         pos_sb = [sb.tile([P, V // PER_COLUMN], U16, name=f"pos_sb{d}") for d in range(D)]
@@ -106,7 +109,7 @@ def tile_picked_dime_silu_p_kernel(
                 nc.vector.tensor_copy(dst[1][:, scalar_m:P], src[:, scalar_m:P, :, 2:4])
             return [quantise(f"{name}_q{u}", grouped[u][:].rearrange("p t m j -> p (t m j)")) for u in range(2)]
 
-        f_sb = [tile(f"f_sb{d}", [P, PACK, V], F32) for d in range(D)]
+        f_sb = [[tile(f"f_sb{d}{u}", [P, 2, V], F32) for u in range(2)] for d in range(D)]
 
         def filters(d, tag):
             a_g = tile(f"a_g{d}", [P, V, PACK], BF16, tag=tag)
@@ -145,7 +148,7 @@ def tile_picked_dime_silu_p_kernel(
 
         def drain(d, f_ps):
             for u in range(2):
-                nc.scalar.copy(f_sb[d][:, 2 * u : 2 * u + 2, :], f_ps[u][:])
+                nc.scalar.copy(f_sb[d][u][:], f_ps[u][:])
 
         w3_q = weights("w3", w3_raw, P)
         drain(0, filters(0, None))
@@ -188,30 +191,55 @@ def tile_picked_dime_silu_p_kernel(
                 layer(z, t, h_ps[t - 1], slice(0, S))
 
         f1_ps = filters(1, None)
-        h = [tile(f"h{t}", [P, S], F32) for t in range(PACK)]
+        h = [tile(f"h{t}", [P, S], F32, tag="w3_q0_codes" if t == 2 else None) for t in range(PACK)]
         for e, cols in enumerate(h0_cols):
             nc.scalar.activation(h[0][:, cols], h0_ps[e][:], SILU)
         for t in range(1, PACK):
             nc.scalar.activation(h[t][:], h_ps[t - 1][:], SILU)
-        drain(1, f1_ps)
+            if t % 2:
+                nc.scalar.copy(f_sb[1][t // 2][:], f1_ps[t // 2][:])
 
-        prod = [tile(f"prod{d}", [P, PACK, V], F32, tag=None if d else "a_raw1") for d in range(D)]
-        for d in range(D):
-            for t in range(PACK):
-                pieces = 2 if (d, t) == (D - 1, PACK - 1) else 1
-                n = V // pieces
-                for s in range(pieces):
-                    cols = slice(n * s, n * (s + 1))
-                    entries = pos_sb[d][:, cols.start // PER_COLUMN : cols.stop // PER_COLUMN]
-                    nc.vector.tensor_tensor(prod[d][:, t, cols], h[t][:].indirect(entries), f_sb[d][:, t, cols], MULT)
+        prod = [
+            [tile(f"prod{d}{u}", [P, 2, V], F32, tag=None if d or u else "a_raw1") for u in range(2)] for d in range(D)
+        ]
+        for u in range(2):
+            for d in range(D):
+                for e in range(2):
+                    pieces = 2 if (u, d, e) == (1, D - 1, 1) else 1
+                    n = V // pieces
+                    for s in range(pieces):
+                        cols = slice(n * s, n * (s + 1))
+                        entries = pos_sb[d][:, cols.start // PER_COLUMN : cols.stop // PER_COLUMN]
+                        nc.vector.tensor_tensor(
+                            prod[d][u][:, e, cols], h[2 * u + e][:].indirect(entries), f_sb[d][u][:, e, cols], MULT
+                        )
 
         z_g = [tile(f"z_g{s}", [P, P, PACK], BF16) for s in range(2)]
         for s in range(2):
             cols = slice(P * s, P * (s + 1))
+            turned = psum.tile([P, 2, P], F32, name=f"turned{s}", tag=f"bank{6 + s}")
+            for e in range(2):
+                for d in range(D):
+                    nc.tensor.matmul(
+                        turned[:, e, :],
+                        prod[d][0][:, e, cols],
+                        ident[:],
+                        start=(d == 0),
+                        stop=(d == D - 1),
+                        is_transpose=True,
+                    )
+            z_pairs = tile(f"z_pairs{s}", [P, P, 2], BF16)
+            nc.scalar.copy(z_pairs[:], turned[:].rearrange("v e p -> v p e"))
+            back = psum.tile([P, P], F32, name=f"back{s}", tag=f"bank{2 + s}")
+            nc.tensor.transpose(back[:], z_pairs[:].rearrange("v p e -> v (p e)").bitcast(F32), ident[:])
+            words = z_g[s][:].rearrange("p v t -> p (v t)").bitcast(F32).rearrange("p (v u) -> p v u", u=2)
+            nc.scalar.copy(words[:, :, 0], back[:])
+        for s in range(2):
+            cols = slice(P * s, P * (s + 1))
             nc.vector.tensor_tensor(
-                z_g[s][:].rearrange("p (c i) t -> p c t i", i=RUN),
-                prod[0][:, :, cols].rearrange("p t (c i) -> p c t i", i=RUN),
-                prod[1][:, :, cols].rearrange("p t (c i) -> p c t i", i=RUN),
+                z_g[s][:, :, 2:4].rearrange("p (c i) t -> p c t i", i=RUN),
+                prod[0][1][:, :, cols].rearrange("p t (c i) -> p c t i", i=RUN),
+                prod[1][1][:, :, cols].rearrange("p t (c i) -> p c t i", i=RUN),
                 ADD,
             )
         for s in range(2):

@@ -47,7 +47,7 @@ def tile_picked_dime_silu_p_kernel(
 
         x_sc = tile("x_sc", [P, T], U8)
         w2_sc = tile("w2_sc", [P, N], U8)
-        nc.vector.memset(x_sc[:].bitcast(I32), 0)
+        nc.gpsimd.memset(x_sc[:].bitcast(I32), 0)
         nc.gpsimd.memset(w2_sc[:].bitcast(I32), 0)
         ident = tile("ident", [P, P], F32)
         make_identity(nc, ident[:])

@@ -1,7 +1,6 @@
 from contextlib import ExitStack
 
 import concourse.mybir as mybir
-from concourse.masks import make_identity
 
 K, T, S, V, H, N, J = 1024, 2048, 512, 256, 512, 128, 512
 D = 2
@@ -15,6 +14,7 @@ U16 = mybir.dt.uint16
 U8 = mybir.dt.uint8
 FP8X4 = mybir.dt.float8_e4m3fn_x4
 SILU = mybir.ActivationFunctionType.Silu
+COPY = mybir.ActivationFunctionType.Copy
 MULT = mybir.AluOpType.mult
 ADD = mybir.AluOpType.add
 
@@ -25,6 +25,8 @@ PASSES = K // K_PASS
 QUADRANTS = 4
 PER_COLUMN = 16
 RUN = 4
+QUARTERS = S // P
+HALVES = V // P
 
 
 def tile_picked_dime_silu_p_kernel(
@@ -38,6 +40,12 @@ def tile_picked_dime_silu_p_kernel(
         def tile(name, shape, dtype, tag=None):
             return sb.tile(shape, dtype, name=name, tag=tag or name, align_bytes=64)
 
+        def piece(n):
+            return slice(P * n, P * (n + 1))
+
+        def entries(offsets, cols):
+            return offsets[:, cols.start // PER_COLUMN : cols.stop // PER_COLUMN]
+
         def quantise(name, grouped):
             width = grouped.shape[1] // PACK
             codes = tile(name + "_codes", [P, width], U32)
@@ -45,12 +53,22 @@ def tile_picked_dime_silu_p_kernel(
             nc.vector.quantize_mx(out=codes[:].bitcast(FP8X4), scales=scales[:], in_=grouped)
             return codes, scales
 
+        def product(acc, left, left_cols, codes, scales, start, stop):
+            nc.tensor.matmul_mx(
+                out=acc,
+                lhsT=left[0][:, left_cols].bitcast(FP8X4),
+                lhsT_scale=left[1][:, left_cols],
+                rhs=codes.bitcast(FP8X4),
+                rhs_scale=scales,
+                start=start,
+                stop=stop,
+            )
+
         x_sc = tile("x_sc", [P, T], U8)
+        xs = tile("xs", [P, PASSES * S], U8)
         w2_sc = tile("w2_sc", [P, N], U8)
-        nc.gpsimd.memset(x_sc[:].bitcast(I32), 0)
-        nc.gpsimd.memset(w2_sc[:].bitcast(I32), 0)
-        ident = tile("ident", [P, P], F32)
-        make_identity(nc, ident[:])
+        for cleared in (x_sc[32:64, :], x_sc[64:P, :], xs[:], w2_sc[:]):
+            nc.gpsimd.memset(cleared.bitcast(I32), 0)
 
         offs_sb = sb.tile([P, S // PER_COLUMN], U16, name="offs_sb")
         pos_sb = [sb.tile([P, V // PER_COLUMN], U16, name=f"pos_sb{d}") for d in range(D)]
@@ -58,6 +76,8 @@ def tile_picked_dime_silu_p_kernel(
         a_raw = [tile(f"a_raw{d}", [P, PACK, V], F32) for d in range(D)]
         w1_raw = [tile(f"w1_raw{z}", [P, PACK, H], F32) for z in range(PASSES)]
         x_wd = [tile(f"x_wd{z}", [P, T], I32) for z in range(PASSES)]
+        xs_rows = tile("xs_rows", [P, S], U8)
+        w2_wd = tile("w2_wd", [P, N], I32)
 
         def load_rows(dst, src):
             nc.sync.dma_start(out=dst[:], in_=src.rearrange("(p j) c -> p j c", j=PACK))
@@ -65,195 +85,118 @@ def tile_picked_dime_silu_p_kernel(
         def load_words(z):
             nc.sync.dma_start(out=x_wd[z][:], in_=x_words[z].rearrange("p n t -> p (n t)").bitcast(I32))
 
-        xs_rows = tile("xs_rows", [P, S], U8)
-        xs = tile("xs", [P, PASSES * S], U8)
-        nc.gpsimd.memset(xs[:].bitcast(I32), 0)
-
-        def place_scales(first, last):
-            for q in range(first, last):
-                nc.sync.dma_start(
-                    out=xs[32 * q : 32 * q + 4, :].bitcast(I32).rearrange("r (z n) -> r z n", z=PASSES),
-                    in_=xs_rows[32 * q : 32 * (q + 1) : 4, :].bitcast(I32),
-                )
-
-        load_rows(a_raw[0], aT[:, 0:V])
-        nc.sync.dma_start(out=x_sc[0:P:4, :].bitcast(I32), in_=x_scales.bitcast(I32).rearrange("z r n -> r z n"))
+        nc.sync.dma_start(out=x_sc[0:32, :].bitcast(I32), in_=x_scales.bitcast(I32).rearrange("z r n -> r z n"))
         nc.sync.dma_start(offs_sb[:], offs)
         nc.vector.tensor_copy(xs_rows[:], x_sc[:].indirect(offs_sb[:]))
-        load_rows(w3_raw, w3)
         load_rows(w1_raw[0], w1[0:K_PASS, :])
         load_words(0)
-        place_scales(0, QUADRANTS - 1)
+        for q in range(QUADRANTS):
+            nc.sync.dma_start(
+                out=xs[32 * q : 32 * q + 4, :].bitcast(I32).rearrange("r (z n) -> r z n", z=PASSES),
+                in_=xs_rows[8 * q : 8 * (q + 1), :].bitcast(I32),
+            )
         load_rows(w1_raw[1], w1[K_PASS : 2 * K_PASS, :])
-        place_scales(QUADRANTS - 1, QUADRANTS)
         load_words(1)
-        load_rows(a_raw[1], aT[:, V : 2 * V])
         nc.sync.dma_start(pos_sb[0][:], pos1)
         nc.sync.dma_start(pos_sb[1][:], pos2)
-        w2_wd = tile("w2_wd", [P, N], I32)
+        load_rows(w3_raw, w3)
+        for d in range(D):
+            load_rows(a_raw[d], aT[:, V * d : V * (d + 1)])
         nc.sync.dma_start(out=w2_wd[:], in_=w2_words[0].rearrange("p n t -> p (n t)").bitcast(I32))
         for q in range(QUADRANTS):
             nc.sync.dma_start(
                 out=w2_sc[32 * q : 32 * q + 4, :].bitcast(I32), in_=w2_scales[0, 4 * q : 4 * q + 4, :].bitcast(I32)
             )
 
-        xw = [tile(f"xw{z}", [P, S], U32) for z in range(PASSES)]
-
-        def weights(name, raw, scalar_m):
+        def weights(name, raw, shared):
             src = raw[:].rearrange("p j (m t) -> p m j t", t=PACK)
             grouped = [tile(f"{name}_g{u}", [P, 2, P, PACK], BF16) for u in range(2)]
             dst = [g[:].rearrange("p t m j -> p m j t") for g in grouped]
-            nc.scalar.copy(dst[1][:, 0:scalar_m], src[:, 0:scalar_m, :, 2:4])
             nc.vector.tensor_copy(dst[0], src[:, :, :, 0:2])
-            if scalar_m < P:
-                nc.vector.tensor_copy(dst[1][:, scalar_m:P], src[:, scalar_m:P, :, 2:4])
+            if shared:
+                nc.scalar.copy(dst[1], src[:, :, :, 2:4])
+            else:
+                nc.vector.tensor_copy(dst[1], src[:, :, :, 2:4])
             return [quantise(f"{name}_q{u}", grouped[u][:].rearrange("p t m j -> p (t m j)")) for u in range(2)]
 
-        f_sb = [[tile(f"f_sb{d}{u}", [P, 2, V], F32) for u in range(2)] for d in range(D)]
-
-        def filters(d, tag):
-            a_g = tile(f"a_g{d}", [P, V, PACK], BF16, tag=tag)
-            a_codes = tile(f"a_codes{d}", [P, V], U32)
-            a_scales = tile(f"a_scales{d}", [P, V], U8)
-            for e in range(2):
-                cols = slice(P * e, P * (e + 1))
-                nc.vector.tensor_copy(
-                    a_g[:, cols, :].rearrange("p (c i) j -> p c j i", i=RUN),
-                    a_raw[d][:, :, cols].rearrange("p j (c i) -> p c j i", i=RUN),
-                )
-            for e in range(2):
-                cols = slice(P * e, P * (e + 1))
-                nc.vector.quantize_mx(
-                    out=a_codes[:, cols].bitcast(FP8X4),
-                    scales=a_scales[:, cols],
-                    in_=a_g[:, cols, :].rearrange("p c j -> p (c j)"),
-                )
-            f_ps = []
-            for u in range(2):
-                bank = psum.tile([P, 2, V], F32, name=f"f_ps{d}{u}", tag=f"bank{PACK + u}")
-                codes, scales = w3_q[u]
-                for e in range(2):
-                    cols = slice(P * e, P * (e + 1))
-                    nc.tensor.matmul_mx(
-                        out=bank[:, e, :],
-                        lhsT=codes[:, cols].bitcast(FP8X4),
-                        lhsT_scale=scales[:, cols],
-                        rhs=a_codes[:].bitcast(FP8X4),
-                        rhs_scale=a_scales[:],
-                        start=True,
-                        stop=True,
-                    )
-                f_ps.append(bank)
-            return f_ps
-
-        def drain(d, f_ps):
-            for u in range(2):
-                nc.scalar.copy(f_sb[d][u][:], f_ps[u][:])
-
-        w3_q = weights("w3", w3_raw, P)
-        drain(0, filters(0, None))
-
-        h_ps = [psum.tile([P, S], F32, name=f"h_ps{t}", tag=f"bank{t}") for t in range(1, PACK)]
-        h0_cols = [slice(0, S // 2), slice(S // 2, 3 * S // 4), slice(3 * S // 4, S)]
-        h0_ps = [
-            psum.tile([P, cols.stop - cols.start], F32, name=f"h0_ps{e}", tag=f"bank{(0, 6, 7)[e]}")
-            for e, cols in enumerate(h0_cols)
-        ]
-        halves = [slice(0, S // 2), slice(S // 2, S)]
-        half_columns = S // 2 // PER_COLUMN
-        w1_q = {}
-
-        def layer(z, t, acc, cols):
-            codes, scales = w1_q[z][t // 2]
-            w_cols = slice(P * (t % 2), P * (t % 2 + 1))
-            nc.tensor.matmul_mx(
-                out=acc[:],
-                lhsT=codes[:, w_cols].bitcast(FP8X4),
-                lhsT_scale=scales[:, w_cols],
-                rhs=xw[z][:, cols].bitcast(FP8X4),
-                rhs_scale=xs[:, S * z + cols.start : S * z + cols.stop],
-                start=(z == 0),
-                stop=(z == PASSES - 1),
-            )
-
+        xw = [tile(f"xw{z}", [P, S], U32) for z in range(PASSES)]
+        h_ps = [psum.tile([P, PACK, P], F32, name=f"h_ps{e}", tag=f"bank{e}") for e in range(QUARTERS)]
+        h = tile("h", [P, PACK, S], F32)
         for z in range(PASSES):
             last = z == PASSES - 1
-            w1_q[z] = weights(f"w1{z}", w1_raw[z], P)
+            w1_q = weights(f"w1{z}", w1_raw[z], True)
             window = x_wd[z][:].bitcast(U32)
             if not last:
                 nc.vector.tensor_copy(xw[z][:], window.indirect(offs_sb[:]))
-            for e, cols in enumerate(h0_cols):
-                if last and e < 2:
-                    entries = offs_sb[:, half_columns * e : half_columns * (e + 1)]
-                    nc.vector.tensor_copy(xw[z][:, halves[e]], window.indirect(entries))
-                layer(z, 0, h0_ps[e], cols)
-            for t in range(1, PACK):
-                layer(z, t, h_ps[t - 1], slice(0, S))
-
-        f1_ps = filters(1, None)
-        h = [tile(f"h{t}", [P, S], F32, tag="w3_q0_codes" if t == 2 else None) for t in range(PACK)]
-        for e, cols in enumerate(h0_cols):
-            nc.scalar.activation(h[0][:, cols], h0_ps[e][:], SILU)
-        for t in range(1, PACK):
-            nc.scalar.activation(h[t][:], h_ps[t - 1][:], SILU)
-            if t % 2:
-                nc.scalar.copy(f_sb[1][t // 2][:], f1_ps[t // 2][:])
-
-        prod = [
-            [tile(f"prod{d}{u}", [P, 2, V], F32, tag=None if d or u else "a_raw1") for u in range(2)] for d in range(D)
-        ]
-        for u in range(2):
-            for d in range(D):
-                for e in range(2):
-                    pieces = 2 if (u, d, e) == (1, D - 1, 1) else 1
-                    n = V // pieces
-                    for s in range(pieces):
-                        cols = slice(n * s, n * (s + 1))
-                        entries = pos_sb[d][:, cols.start // PER_COLUMN : cols.stop // PER_COLUMN]
-                        nc.vector.tensor_tensor(
-                            prod[d][u][:, e, cols], h[2 * u + e][:].indirect(entries), f_sb[d][u][:, e, cols], MULT
-                        )
-
-        z_g = [tile(f"z_g{s}", [P, P, PACK], BF16) for s in range(2)]
-        for s in range(2):
-            cols = slice(P * s, P * (s + 1))
-            turned = psum.tile([P, 2, P], F32, name=f"turned{s}", tag=f"bank{6 + s}")
-            for e in range(2):
-                for d in range(D):
-                    nc.tensor.matmul(
-                        turned[:, e, :],
-                        prod[d][0][:, e, cols],
-                        ident[:],
-                        start=(d == 0),
-                        stop=(d == D - 1),
-                        is_transpose=True,
+            for e in range(QUARTERS):
+                cols = piece(e)
+                if last:
+                    nc.vector.tensor_copy(xw[z][:, cols], window.indirect(entries(offs_sb, cols)))
+                for t in range(PACK):
+                    product(
+                        h_ps[e][:, t, :],
+                        w1_q[t // 2],
+                        piece(t % 2),
+                        xw[z][:, cols],
+                        xs[:, S * z + cols.start : S * z + cols.stop],
+                        z == 0 and t == 0,
+                        last and t == PACK - 1,
                     )
-            z_pairs = tile(f"z_pairs{s}", [P, P, 2], BF16)
-            nc.scalar.copy(z_pairs[:], turned[:].rearrange("v e p -> v p e"))
-            back = psum.tile([P, P], F32, name=f"back{s}", tag=f"bank{2 + s}")
-            nc.tensor.transpose(back[:], z_pairs[:].rearrange("v p e -> v (p e)").bitcast(F32), ident[:])
-            words = z_g[s][:].rearrange("p v t -> p (v t)").bitcast(F32).rearrange("p (v u) -> p v u", u=2)
-            nc.scalar.copy(words[:, :, 0], back[:])
-        for s in range(2):
-            cols = slice(P * s, P * (s + 1))
+                if last:
+                    nc.scalar.activation(h[:, :, cols], h_ps[e][:], SILU)
+
+        picked = [tile(f"picked{d}", [P, PACK, V], F32) for d in range(D)]
+        for d, cols in [(0, slice(0, V))] + [(1, piece(s)) for s in range(HALVES)]:
+            for t in range(PACK):
+                nc.scalar.activation(picked[d][:, t, cols], h[:, t, :].indirect(entries(pos_sb[d], cols)), COPY)
+
+        w3_q = weights("w3", w3_raw, False)
+        f_ps = []
+        for d in range(D):
+            a_g = tile(f"a_g{d}", [P, V, PACK], BF16)
+            for s in range(HALVES):
+                nc.vector.tensor_copy(
+                    a_g[:, piece(s), :].rearrange("p (c i) j -> p c j i", i=RUN),
+                    a_raw[d][:, :, piece(s)].rearrange("p j (c i) -> p c j i", i=RUN),
+                )
+            banks = []
+            for s in range(HALVES):
+                codes, scales = quantise(f"a_q{d}{s}", a_g[:, piece(s), :].rearrange("p c j -> p (c j)"))
+                bank = psum.tile([P, PACK, P], F32, name=f"f_ps{d}{s}", tag=f"bank{QUARTERS + 2 * d + s}")
+                for t in range(PACK):
+                    product(bank[:, t, :], w3_q[t // 2], piece(t % 2), codes[:], scales[:], True, True)
+                banks.append(bank)
+            f_ps.append(banks)
+
+        prod = [[tile(f"prod{d}{s}", [P, PACK, P], F32) for s in range(HALVES)] for d in range(D)]
+        z_g = [tile(f"z_g{s}", [P, P, PACK], BF16) for s in range(HALVES)]
+
+        def multiply(d, s, rows):
+            nc.vector.tensor_tensor(prod[d][s][:, rows, :], picked[d][:, rows, piece(s)], f_ps[d][s][:, rows, :], MULT)
+
+        def add(s):
             nc.vector.tensor_tensor(
-                z_g[s][:, :, 2:4].rearrange("p (c i) t -> p c t i", i=RUN),
-                prod[0][1][:, :, cols].rearrange("p t (c i) -> p c t i", i=RUN),
-                prod[1][1][:, :, cols].rearrange("p t (c i) -> p c t i", i=RUN),
+                z_g[s][:].rearrange("p (c i) t -> p c t i", i=RUN),
+                prod[0][s][:].rearrange("p t (c i) -> p c t i", i=RUN),
+                prod[1][s][:].rearrange("p t (c i) -> p c t i", i=RUN),
                 ADD,
             )
-        for s in range(2):
-            z_codes, z_scales = quantise(f"z_q{s}", z_g[s][:].rearrange("p v t -> p (v t)"))
+
+        def project(s):
+            codes, scales = quantise(f"z_q{s}", z_g[s][:].rearrange("p v t -> p (v t)"))
             o_ps = psum.tile([P, P], F32, name=f"o_ps{s}", tag=f"bank{s}")
-            nc.tensor.matmul_mx(
-                out=o_ps[:],
-                lhsT=w2_wd[:].bitcast(FP8X4),
-                lhsT_scale=w2_sc[:],
-                rhs=z_codes[:].bitcast(FP8X4),
-                rhs_scale=z_scales[:],
-                start=True,
-                stop=True,
-            )
+            product(o_ps[:], (w2_wd, w2_sc), piece(0), codes[:], scales[:], True, True)
             o_sb = tile(f"o_sb{s}", [P, P], F32)
             nc.scalar.activation(o_sb[:], o_ps[:], SILU)
-            nc.sync.dma_start(out=out[:, P * s : P * (s + 1)], in_=o_sb[:])
+            nc.sync.dma_start(out=out[:, piece(s)], in_=o_sb[:])
+
+        every = slice(0, PACK)
+        multiply(0, 0, every)
+        multiply(0, 1, every)
+        multiply(1, 0, every)
+        add(0)
+        multiply(1, 1, slice(0, PACK - 1))
+        project(0)
+        multiply(1, 1, slice(PACK - 1, PACK))
+        add(1)
+        project(1)

@@ -72,8 +72,8 @@ def tile_picked_dime_silu_p_kernel(
 
         offs_sb = sb.tile([P, S // PER_COLUMN], U16, name="offs_sb")
         pos_sb = [sb.tile([P, V // PER_COLUMN], U16, name=f"pos_sb{d}") for d in range(D)]
-        w3_raw = tile("w3_raw", [P, PACK, H], F32)
-        a_raw = [tile(f"a_raw{d}", [P, PACK, V], F32) for d in range(D)]
+        w3_raw = [tile(f"w3_raw{e}", [P, PACK, H // 2], F32) for e in range(2)]
+        a_raw = tile("a_raw", [P, PACK, D * V], F32)
         w1_raw = [tile(f"w1_raw{z}", [P, PACK, H], F32) for z in range(PASSES)]
         x_wd = [tile(f"x_wd{z}", [P, T], I32) for z in range(PASSES)]
         xs_rows = tile("xs_rows", [P, S], U8)
@@ -97,26 +97,23 @@ def tile_picked_dime_silu_p_kernel(
             )
         load_rows(w1_raw[1], w1[K_PASS : 2 * K_PASS, :])
         load_words(1)
+        for e in range(2):
+            load_rows(w3_raw[e], w3[:, H // 2 * e : H // 2 * (e + 1)])
         nc.sync.dma_start(pos_sb[0][:], pos1)
         nc.sync.dma_start(pos_sb[1][:], pos2)
-        load_rows(w3_raw, w3)
-        for d in range(D):
-            load_rows(a_raw[d], aT[:, V * d : V * (d + 1)])
+        load_rows(a_raw, aT)
         nc.sync.dma_start(out=w2_wd[:], in_=w2_words[0].rearrange("p n t -> p (n t)").bitcast(I32))
         for q in range(QUADRANTS):
             nc.sync.dma_start(
                 out=w2_sc[32 * q : 32 * q + 4, :].bitcast(I32), in_=w2_scales[0, 4 * q : 4 * q + 4, :].bitcast(I32)
             )
 
-        def weights(name, raw, shared):
+        def weights(name, raw):
             src = raw[:].rearrange("p j (m t) -> p m j t", t=PACK)
             grouped = [tile(f"{name}_g{u}", [P, 2, P, PACK], BF16) for u in range(2)]
             dst = [g[:].rearrange("p t m j -> p m j t") for g in grouped]
             nc.vector.tensor_copy(dst[0], src[:, :, :, 0:2])
-            if shared:
-                nc.scalar.copy(dst[1], src[:, :, :, 2:4])
-            else:
-                nc.vector.tensor_copy(dst[1], src[:, :, :, 2:4])
+            nc.scalar.copy(dst[1], src[:, :, :, 2:4])
             return [quantise(f"{name}_q{u}", grouped[u][:].rearrange("p t m j -> p (t m j)")) for u in range(2)]
 
         xw = [tile(f"xw{z}", [P, S], U32) for z in range(PASSES)]
@@ -124,7 +121,7 @@ def tile_picked_dime_silu_p_kernel(
         h = tile("h", [P, PACK, S], F32)
         for z in range(PASSES):
             last = z == PASSES - 1
-            w1_q = weights(f"w1{z}", w1_raw[z], True)
+            w1_q = weights(f"w1{z}", w1_raw[z])
             window = x_wd[z][:].bitcast(U32)
             if not last:
                 nc.vector.tensor_copy(xw[z][:], window.indirect(offs_sb[:]))
@@ -145,28 +142,54 @@ def tile_picked_dime_silu_p_kernel(
                 if last:
                     nc.scalar.activation(h[:, :, cols], h_ps[e][:], SILU)
 
-        picked = [tile(f"picked{d}", [P, PACK, V], F32) for d in range(D)]
-        for d, cols in [(0, slice(0, V))] + [(1, piece(s)) for s in range(HALVES)]:
-            for t in range(PACK):
-                nc.scalar.activation(picked[d][:, t, cols], h[:, t, :].indirect(entries(pos_sb[d], cols)), COPY)
+        w3_g = tile("w3_g", [P, PACK, P, PACK], BF16)
+        w3_dst = w3_g[:].rearrange("p t m j -> p m j t")
+        w3_src = [raw[:].rearrange("p j (m t) -> p m j t", t=PACK) for raw in w3_raw]
+        nc.vector.tensor_copy(w3_dst[:, 0 : P // 2], w3_src[0])
+        for u in range(2):
+            nc.vector.tensor_copy(w3_dst[:, P // 2 : P, :, 2 * u : 2 * u + 2], w3_src[1][:, :, :, 2 * u : 2 * u + 2])
+        w3_q = [
+            quantise(f"w3_q{u}", w3_g[:, 2 * u : 2 * u + 2].rearrange("p t m j -> p (t m j)")) for u in range(2)
+        ]
 
-        w3_q = weights("w3", w3_raw, False)
-        f_ps = []
-        for d in range(D):
-            a_g = tile(f"a_g{d}", [P, V, PACK], BF16)
-            for s in range(HALVES):
-                nc.vector.tensor_copy(
-                    a_g[:, piece(s), :].rearrange("p (c i) j -> p c j i", i=RUN),
-                    a_raw[d][:, :, piece(s)].rearrange("p j (c i) -> p c j i", i=RUN),
-                )
-            banks = []
-            for s in range(HALVES):
-                codes, scales = quantise(f"a_q{d}{s}", a_g[:, piece(s), :].rearrange("p c j -> p (c j)"))
-                bank = psum.tile([P, PACK, P], F32, name=f"f_ps{d}{s}", tag=f"bank{QUARTERS + 2 * d + s}")
-                for t in range(PACK):
-                    product(bank[:, t, :], w3_q[t // 2], piece(t % 2), codes[:], scales[:], True, True)
-                banks.append(bank)
-            f_ps.append(banks)
+        picked = [tile(f"picked{d}", [P, PACK, V], F32) for d in range(D)]
+        whole = slice(0, V)
+
+        def operands(d, t, cols):
+            return picked[d][:, t, cols], h[:, t, :].indirect(entries(pos_sb[d], cols))
+
+        nc.vector.tensor_copy(*operands(0, 0, whole))
+        nc.vector.tensor_copy(*operands(0, 1, piece(0)))
+        for t in (2, 3):
+            nc.scalar.activation(*operands(0, t, whole), COPY)
+        for t in range(PACK):
+            nc.scalar.activation(*operands(1, t, piece(0)), COPY)
+        nc.scalar.activation(*operands(0, 1, piece(1)), COPY)
+        for t in range(PACK):
+            nc.scalar.activation(*operands(1, t, piece(1)), COPY)
+
+        parts = [(d, s) for s in range(HALVES) for d in range(D)]
+        a_g = {part: tile(f"a_g{part[0]}{part[1]}", [P, P, PACK], BF16) for part in parts}
+        f_ps = [[None] * HALVES for d in range(D)]
+
+        def round_angles(d, s):
+            nc.vector.tensor_copy(
+                a_g[d, s][:].rearrange("p (c i) j -> p c j i", i=RUN),
+                a_raw[:, :, piece(HALVES * d + s)].rearrange("p j (c i) -> p c j i", i=RUN),
+            )
+
+        def filters(d, s):
+            codes, scales = quantise(f"a_q{d}{s}", a_g[d, s][:].rearrange("p c j -> p (c j)"))
+            bank = psum.tile([P, PACK, P], F32, name=f"f_ps{d}{s}", tag=f"bank{QUARTERS + 2 * d + s}")
+            for t in range(PACK):
+                product(bank[:, t, :], w3_q[t // 2], piece(t % 2), codes[:], scales[:], True, True)
+            f_ps[d][s] = bank
+
+        round_angles(*parts[0])
+        for n, part in enumerate(parts):
+            if n + 1 < len(parts):
+                round_angles(*parts[n + 1])
+            filters(*part)
 
         prod = [[tile(f"prod{d}{s}", [P, PACK, P], F32) for s in range(HALVES)] for d in range(D)]
         z_g = [tile(f"z_g{s}", [P, P, PACK], BF16) for s in range(HALVES)]
@@ -192,8 +215,8 @@ def tile_picked_dime_silu_p_kernel(
 
         every = slice(0, PACK)
         multiply(0, 0, every)
-        multiply(0, 1, every)
         multiply(1, 0, every)
+        multiply(0, 1, every)
         add(0)
         multiply(1, 1, slice(0, PACK - 1))
         project(0)

@@ -73,7 +73,7 @@ def tile_picked_dime_silu_p_kernel(
         offs_sb = sb.tile([P, S // PER_COLUMN], U16, name="offs_sb")
         pos_sb = [sb.tile([P, V // PER_COLUMN], U16, name=f"pos_sb{d}") for d in range(D)]
         w3_raw = [tile(f"w3_raw{e}", [P, PACK, H // 2], F32) for e in range(2)]
-        a_raw = tile("a_raw", [P, PACK, D * V], F32)
+        a_raw = [tile(f"a_raw{d}", [P, PACK, V], F32) for d in range(D)]
         w1_raw = [tile(f"w1_raw{z}", [P, PACK, H], F32) for z in range(PASSES)]
         x_wd = [tile(f"x_wd{z}", [P, T], I32) for z in range(PASSES)]
         xs_rows = tile("xs_rows", [P, S], U8)
@@ -101,7 +101,8 @@ def tile_picked_dime_silu_p_kernel(
             load_rows(w3_raw[e], w3[:, H // 2 * e : H // 2 * (e + 1)])
         nc.sync.dma_start(pos_sb[0][:], pos1)
         nc.sync.dma_start(pos_sb[1][:], pos2)
-        load_rows(a_raw, aT)
+        for d in range(D):
+            load_rows(a_raw[d], aT[:, V * d : V * (d + 1)])
         nc.sync.dma_start(out=w2_wd[:], in_=w2_words[0].rearrange("p n t -> p (n t)").bitcast(I32))
         for q in range(QUADRANTS):
             nc.sync.dma_start(
@@ -152,56 +153,35 @@ def tile_picked_dime_silu_p_kernel(
             quantise(f"w3_q{u}", w3_g[:, 2 * u : 2 * u + 2].rearrange("p t m j -> p (t m j)")) for u in range(2)
         ]
 
-        picked = [tile(f"picked{d}", [P, PACK, V], F32) for d in range(D)]
         whole = slice(0, V)
+        every = slice(0, PACK)
+        a_g = [[tile(f"a_g{d}{s}", [P, P, PACK], BF16) for s in range(HALVES)] for d in range(D)]
+        z_g = [tile(f"z_g{s}", [P, P, PACK], BF16) for s in range(HALVES)]
+        f_ps = {}
 
-        def operands(d, t, cols):
-            return picked[d][:, t, cols], h[:, t, :].indirect(entries(pos_sb[d], cols))
-
-        nc.vector.tensor_copy(*operands(0, 0, whole))
-        nc.vector.tensor_copy(*operands(0, 1, piece(0)))
-        for t in (2, 3):
-            nc.scalar.activation(*operands(0, t, whole), COPY)
-        for t in range(PACK):
-            nc.scalar.activation(*operands(1, t, piece(0)), COPY)
-        nc.scalar.activation(*operands(0, 1, piece(1)), COPY)
-        for t in range(PACK):
-            nc.scalar.activation(*operands(1, t, piece(1)), COPY)
-
-        parts = [(d, s) for s in range(HALVES) for d in range(D)]
-        a_g = {part: tile(f"a_g{part[0]}{part[1]}", [P, P, PACK], BF16) for part in parts}
-        f_ps = [[None] * HALVES for d in range(D)]
+        def window(d, t, cols):
+            return h[:, t, :].indirect(entries(pos_sb[d], cols))
 
         def round_angles(d, s):
             nc.vector.tensor_copy(
-                a_g[d, s][:].rearrange("p (c i) j -> p c j i", i=RUN),
-                a_raw[:, :, piece(HALVES * d + s)].rearrange("p j (c i) -> p c j i", i=RUN),
+                a_g[d][s][:].rearrange("p (c i) j -> p c j i", i=RUN),
+                a_raw[d][:, :, piece(s)].rearrange("p j (c i) -> p c j i", i=RUN),
             )
 
         def filters(d, s):
-            codes, scales = quantise(f"a_q{d}{s}", a_g[d, s][:].rearrange("p c j -> p (c j)"))
-            bank = psum.tile([P, PACK, P], F32, name=f"f_ps{d}{s}", tag=f"bank{QUARTERS + 2 * d + s}")
+            codes, scales = quantise(f"a_q{d}{s}", a_g[d][s][:].rearrange("p c j -> p (c j)"))
+            f_ps[d, s] = psum.tile([P, PACK, P], F32, name=f"f_ps{d}{s}", tag=f"bank{QUARTERS + 2 * d + s}")
             for t in range(PACK):
-                product(bank[:, t, :], w3_q[t // 2], piece(t % 2), codes[:], scales[:], True, True)
-            f_ps[d][s] = bank
+                product(f_ps[d, s][:, t, :], w3_q[t // 2], piece(t % 2), codes[:], scales[:], True, True)
 
-        round_angles(*parts[0])
-        for n, part in enumerate(parts):
-            if n + 1 < len(parts):
-                round_angles(*parts[n + 1])
-            filters(*part)
-
-        prod = [[tile(f"prod{d}{s}", [P, PACK, P], F32) for s in range(HALVES)] for d in range(D)]
-        z_g = [tile(f"z_g{s}", [P, P, PACK], BF16) for s in range(HALVES)]
-
-        def multiply(d, s, rows):
-            nc.vector.tensor_tensor(prod[d][s][:, rows, :], picked[d][:, rows, piece(s)], f_ps[d][s][:, rows, :], MULT)
+        def multiply(d, s, picked, rows):
+            nc.vector.tensor_tensor(prod[d][s][:, rows, :], picked[:, rows, :], f_ps[d, s][:, rows, :], MULT)
 
         def add(s):
             nc.vector.tensor_tensor(
                 z_g[s][:].rearrange("p (c i) t -> p c t i", i=RUN),
-                prod[0][s][:].rearrange("p t (c i) -> p c t i", i=RUN),
-                prod[1][s][:].rearrange("p t (c i) -> p c t i", i=RUN),
+                prod[0][s].rearrange("p t (c i) -> p c t i", i=RUN),
+                prod[1][s].rearrange("p t (c i) -> p c t i", i=RUN),
                 ADD,
             )
 
@@ -213,13 +193,28 @@ def tile_picked_dime_silu_p_kernel(
             nc.scalar.activation(o_sb[:], o_ps[:], SILU)
             nc.sync.dma_start(out=out[:, piece(s)], in_=o_sb[:])
 
-        every = slice(0, PACK)
-        multiply(0, 0, every)
-        multiply(1, 0, every)
-        multiply(0, 1, every)
+        first = tile("first", [P, PACK, V], F32)
+        second = tile("second", [P, PACK, V], F32)
+        nc.vector.tensor_copy(first[:, 0, :], window(0, 0, whole))
+        for t in range(1, PACK):
+            nc.scalar.activation(first[:, t, :], window(0, t, whole), COPY)
+        for s in range(HALVES):
+            for t in range(PACK):
+                nc.scalar.activation(second[:, t, piece(s)], window(1, t, piece(s)), COPY)
+        for d in range(D):
+            for s in range(HALVES):
+                round_angles(d, s)
+            for s in range(HALVES):
+                filters(d, s)
+        first_prod = tile("first_prod", [P, HALVES, PACK, P], F32, tag="a_raw1")
+        prod = [[first_prod[:, s] for s in range(HALVES)], [tile(f"prod{s}", [P, PACK, P], F32)[:] for s in range(HALVES)]]
+        multiply(0, 0, first[:, :, piece(0)], every)
+        multiply(0, 1, first[:, :, piece(1)], every)
+        multiply(1, 0, second[:, :, piece(0)], every)
+        multiply(1, 1, second[:, :, piece(1)], slice(0, PACK // 2))
         add(0)
-        multiply(1, 1, slice(0, PACK - 1))
+        multiply(1, 1, second[:, :, piece(1)], slice(PACK // 2, PACK - 1))
         project(0)
-        multiply(1, 1, slice(PACK - 1, PACK))
+        multiply(1, 1, second[:, :, piece(1)], slice(PACK - 1, PACK))
         add(1)
         project(1)

@@ -72,7 +72,7 @@ def tile_picked_dime_silu_p_kernel(
 
         offs_sb = sb.tile([P, S // PER_COLUMN], U16, name="offs_sb")
         pos_sb = [sb.tile([P, V // PER_COLUMN], U16, name=f"pos_sb{d}") for d in range(D)]
-        w3_raw = [tile(f"w3_raw{e}", [P, PACK, H // 2], F32) for e in range(2)]
+        w3_raw = [tile(f"w3_raw{e}", [P, PACK // 2, H], F32) for e in range(2)]
         a_raw = [tile(f"a_raw{d}", [P, PACK, V], F32) for d in range(D)]
         w1_raw = [tile(f"w1_raw{z}", [P, PACK, H], F32) for z in range(PASSES)]
         x_wd = [tile(f"x_wd{z}", [P, T], I32) for z in range(PASSES)]
@@ -98,7 +98,7 @@ def tile_picked_dime_silu_p_kernel(
         load_rows(w1_raw[1], w1[K_PASS : 2 * K_PASS, :])
         load_words(1)
         for e in range(2):
-            load_rows(w3_raw[e], w3[:, H // 2 * e : H // 2 * (e + 1)])
+            nc.sync.dma_start(out=w3_raw[e][:], in_=w3.rearrange("(p j) c -> p j c", j=PACK)[:, 2 * e : 2 * e + 2, :])
         nc.sync.dma_start(pos_sb[0][:], pos1)
         nc.sync.dma_start(pos_sb[1][:], pos2)
         for d in range(D):
@@ -144,11 +144,11 @@ def tile_picked_dime_silu_p_kernel(
                     nc.scalar.activation(h[:, :, cols], h_ps[e][:], SILU)
 
         w3_g = tile("w3_g", [P, PACK, P, PACK], BF16)
-        w3_dst = w3_g[:].rearrange("p t m j -> p m j t")
-        w3_src = [raw[:].rearrange("p j (m t) -> p m j t", t=PACK) for raw in w3_raw]
-        nc.vector.tensor_copy(w3_dst[:, 0 : P // 2], w3_src[0])
+        w3_dst = w3_g[:].rearrange("p t m j -> p m t j")
+        w3_src = [raw[:].rearrange("p j (m t) -> p m t j", t=PACK) for raw in w3_raw]
+        nc.vector.tensor_copy(w3_dst[:, :, :, 0:2], w3_src[0])
         for u in range(2):
-            nc.vector.tensor_copy(w3_dst[:, P // 2 : P, :, 2 * u : 2 * u + 2], w3_src[1][:, :, :, 2 * u : 2 * u + 2])
+            nc.vector.tensor_copy(w3_dst[:, :, 2 * u : 2 * u + 2, 2:4], w3_src[1][:, :, 2 * u : 2 * u + 2, :])
         w3_q = [
             quantise(f"w3_q{u}", w3_g[:, 2 * u : 2 * u + 2].rearrange("p t m j -> p (t m j)")) for u in range(2)
         ]
@@ -193,7 +193,7 @@ def tile_picked_dime_silu_p_kernel(
             nc.scalar.activation(o_sb[:], o_ps[:], SILU)
             nc.sync.dma_start(out=out[:, piece(s)], in_=o_sb[:])
 
-        first = tile("first", [P, PACK, V], F32)
+        first = tile("first", [P, PACK, V], F32, tag="w3_raw1")
         second = tile("second", [P, PACK, V], F32)
         nc.vector.tensor_copy(first[:, 0, :], window(0, 0, whole))
         for t in range(1, PACK):

@@ -118,30 +118,31 @@ def tile_picked_dime_silu_p_kernel(
             return [quantise(f"{name}_q{u}", grouped[u][:].rearrange("p t m j -> p (t m j)")) for u in range(2)]
 
         xw = [tile(f"xw{z}", [P, S], U32) for z in range(PASSES)]
-        h_ps = [psum.tile([P, PACK, P], F32, name=f"h_ps{e}", tag=f"bank{e}") for e in range(QUARTERS)]
         h = tile("h", [P, PACK, S], F32)
+        groups = [(0, range(0, 2)), (0, range(2, PACK))] + [(e, range(PACK)) for e in range(1, QUARTERS)]
+        h_ps = [psum.tile([P, len(rows), P], F32, name=f"h_ps{n}", tag=f"bank{n}") for n, (e, rows) in enumerate(groups)]
         for z in range(PASSES):
             last = z == PASSES - 1
             w1_q = weights(f"w1{z}", w1_raw[z])
             window = x_wd[z][:].bitcast(U32)
             if not last:
                 nc.vector.tensor_copy(xw[z][:], window.indirect(offs_sb[:]))
-            for e in range(QUARTERS):
+            for bank, (e, rows) in zip(h_ps, groups):
                 cols = piece(e)
-                if last:
+                if last and rows.start == 0:
                     nc.vector.tensor_copy(xw[z][:, cols], window.indirect(entries(offs_sb, cols)))
-                for t in range(PACK):
+                for t in rows:
                     product(
-                        h_ps[e][:, t, :],
+                        bank[:, t - rows.start, :],
                         w1_q[t // 2],
                         piece(t % 2),
                         xw[z][:, cols],
                         xs[:, S * z + cols.start : S * z + cols.stop],
-                        z == 0 and t == 0,
-                        last and t == PACK - 1,
+                        z == 0 and t == rows.start,
+                        last and t == rows.stop - 1,
                     )
                 if last:
-                    nc.scalar.activation(h[:, :, cols], h_ps[e][:], SILU)
+                    nc.scalar.activation(h[:, rows.start : rows.stop, cols], bank[:], SILU)
 
         w3_g = tile("w3_g", [P, PACK, P, PACK], BF16)
         w3_dst = w3_g[:].rearrange("p t m j -> p m t j")
@@ -177,16 +178,23 @@ def tile_picked_dime_silu_p_kernel(
         def multiply(d, s, picked, rows):
             nc.vector.tensor_tensor(prod[d][s][:, rows, :], picked[:, rows, :], f_ps[d, s][:, rows, :], MULT)
 
-        def add(s):
+        def add(s, cols):
             nc.vector.tensor_tensor(
-                z_g[s][:].rearrange("p (c i) t -> p c t i", i=RUN),
-                prod[0][s].rearrange("p t (c i) -> p c t i", i=RUN),
-                prod[1][s].rearrange("p t (c i) -> p c t i", i=RUN),
+                z_g[s][:, cols, :].rearrange("p (c i) t -> p c t i", i=RUN),
+                prod[0][s][:, :, cols].rearrange("p t (c i) -> p c t i", i=RUN),
+                prod[1][s][:, :, cols].rearrange("p t (c i) -> p c t i", i=RUN),
                 ADD,
             )
 
-        def project(s):
-            codes, scales = quantise(f"z_q{s}", z_g[s][:].rearrange("p v t -> p (v t)"))
+        def project(s, parts):
+            codes = tile(f"z_codes{s}", [P, P], U32)
+            scales = tile(f"z_scales{s}", [P, P], U8)
+            for cols in parts:
+                nc.vector.quantize_mx(
+                    out=codes[:, cols].bitcast(FP8X4),
+                    scales=scales[:, cols],
+                    in_=z_g[s][:, cols, :].rearrange("p v t -> p (v t)"),
+                )
             o_ps = psum.tile([P, P], F32, name=f"o_ps{s}", tag=f"bank{s}")
             product(o_ps[:], (w2_wd, w2_sc), piece(0), codes[:], scales[:], True, True)
             o_sb = tile(f"o_sb{s}", [P, P], F32)
@@ -198,9 +206,10 @@ def tile_picked_dime_silu_p_kernel(
         nc.vector.tensor_copy(first[:, 0, :], window(0, 0, whole))
         for t in range(1, PACK):
             nc.scalar.activation(first[:, t, :], window(0, t, whole), COPY)
-        for s in range(HALVES):
-            for t in range(PACK):
-                nc.scalar.activation(second[:, t, piece(s)], window(1, t, piece(s)), COPY)
+        ends = [slice(P, P + P // 2), slice(P + P // 2, V)]
+        order = [(0, whole)] + [(t, piece(s)) for s in range(HALVES) for t in range(1, PACK)][:-1]
+        for t, cols in order + [(PACK - 1, cols) for cols in ends]:
+            nc.scalar.activation(second[:, t, cols], window(1, t, cols), COPY)
         for d in range(D):
             for s in range(HALVES):
                 round_angles(d, s)
@@ -212,9 +221,14 @@ def tile_picked_dime_silu_p_kernel(
         multiply(0, 1, first[:, :, piece(1)], every)
         multiply(1, 0, second[:, :, piece(0)], every)
         multiply(1, 1, second[:, :, piece(1)], slice(0, PACK // 2))
-        add(0)
+        add(0, piece(0))
         multiply(1, 1, second[:, :, piece(1)], slice(PACK // 2, PACK - 1))
-        project(0)
-        multiply(1, 1, second[:, :, piece(1)], slice(PACK - 1, PACK))
-        add(1)
-        project(1)
+        project(0, [piece(0)])
+        inner = [slice(0, P // 2), slice(P // 2, P)]
+        for cols, here in zip(ends, inner):
+            nc.vector.tensor_tensor(
+                prod[1][1][:, PACK - 1, here], second[:, PACK - 1, cols], f_ps[1, 1][:, PACK - 1, here], MULT
+            )
+        for here in inner:
+            add(1, here)
+        project(1, inner)

@@ -207,7 +207,7 @@ def tile_picked_dime_silu_p_kernel(
         for t in range(1, PACK):
             nc.scalar.activation(first[:, t, :], window(0, t, whole), COPY)
         ends = [slice(P, P + P // 2), slice(P + P // 2, V)]
-        order = [(0, whole)] + [(t, piece(s)) for s in range(HALVES) for t in range(1, PACK)][:-1]
+        order = [(t, piece(s)) for s in range(HALVES) for t in range(PACK)][:-1]
         for t, cols in order + [(PACK - 1, cols) for cols in ends]:
             nc.scalar.activation(second[:, t, cols], window(1, t, cols), COPY)
         for d in range(D):
@@ -219,11 +219,12 @@ def tile_picked_dime_silu_p_kernel(
         prod = [[first_prod[:, s] for s in range(HALVES)], [tile(f"prod{s}", [P, PACK, P], F32)[:] for s in range(HALVES)]]
         multiply(0, 0, first[:, :, piece(0)], every)
         multiply(0, 1, first[:, :, piece(1)], every)
-        multiply(1, 0, second[:, :, piece(0)], every)
-        multiply(1, 1, second[:, :, piece(1)], slice(0, PACK // 2))
+        multiply(1, 0, second[:, :, piece(0)], slice(0, PACK - 1))
+        multiply(1, 0, second[:, :, piece(0)], slice(PACK - 1, PACK))
         add(0, piece(0))
-        multiply(1, 1, second[:, :, piece(1)], slice(PACK // 2, PACK - 1))
+        multiply(1, 1, second[:, :, piece(1)], slice(0, PACK // 2))
         project(0, [piece(0)])
+        multiply(1, 1, second[:, :, piece(1)], slice(PACK // 2, PACK - 1))
         inner = [slice(0, P // 2), slice(P // 2, P)]
         for cols, here in zip(ends, inner):
             nc.vector.tensor_tensor(

@@ -195,10 +195,11 @@ def tile_picked_dime_silu_p_kernel(
                     scales=scales[:, cols],
                     in_=z_g[s][:, cols, :].rearrange("p v t -> p (v t)"),
                 )
-            o_ps = psum.tile([P, P], F32, name=f"o_ps{s}", tag=f"bank{s}")
-            product(o_ps[:], (w2_wd, w2_sc), piece(0), codes[:], scales[:], True, True)
             o_sb = tile(f"o_sb{s}", [P, P], F32)
-            nc.scalar.activation(o_sb[:], o_ps[:], SILU)
+            for n, cols in enumerate(parts):
+                o_ps = psum.tile([P, cols.stop - cols.start], F32, name=f"o_ps{s}{n}", tag=f"bank{s + n}")
+                product(o_ps[:], (w2_wd, w2_sc), piece(0), codes[:, cols], scales[:, cols], True, True)
+                nc.scalar.activation(o_sb[:, cols], o_ps[:], SILU)
             nc.sync.dma_start(out=out[:, piece(s)], in_=o_sb[:])
 
         first = tile("first", [P, PACK, V], F32, tag="w3_raw1")

from contextlib import ExitStack

import concourse.mybir as mybir

K, T, S, V, H, N, J = 1024, 2048, 512, 256, 512, 128, 512
D = 2
FLOPS = 2 * K * H * S + 2 * J * H * D * V + 2 * H * N * V

F32 = mybir.dt.float32
BF16 = mybir.dt.bfloat16
I32 = mybir.dt.int32
U32 = mybir.dt.uint32
U16 = mybir.dt.uint16
U8 = mybir.dt.uint8
FP8X4 = mybir.dt.float8_e4m3fn_x4
SILU = mybir.ActivationFunctionType.Silu
COPY = mybir.ActivationFunctionType.Copy
MULT = mybir.AluOpType.mult
ADD = mybir.AluOpType.add

P = 128
PACK = 4
K_PASS = P * PACK
PASSES = K // K_PASS
QUADRANTS = 4
PER_COLUMN = 16
RUN = 4
QUARTERS = S // P
HALVES = V // P


def tile_picked_dime_silu_p_kernel(
    tc, x_words, x_scales, aT, w1, w3, w2_words, w2_scales, offs, pos1, pos2, out
):
    nc = tc.nc
    with ExitStack() as ctx:
        sb = ctx.enter_context(tc.tile_pool(name="sb", bufs=1))
        psum = ctx.enter_context(tc.psum_pool(name="psum", bufs=1))

        def tile(name, shape, dtype, tag=None):
            return sb.tile(shape, dtype, name=name, tag=tag or name, align_bytes=64)

        def piece(n):
            return slice(P * n, P * (n + 1))

        def entries(offsets, cols):
            return offsets[:, cols.start // PER_COLUMN : cols.stop // PER_COLUMN]

        def quantise(name, grouped):
            width = grouped.shape[1] // PACK
            codes = tile(name + "_codes", [P, width], U32)
            scales = tile(name + "_scales", [P, width], U8)
            nc.vector.quantize_mx(out=codes[:].bitcast(FP8X4), scales=scales[:], in_=grouped)
            return codes, scales

        def product(acc, left, left_cols, codes, scales, start, stop):
            nc.tensor.matmul_mx(
                out=acc,
                lhsT=left[0][:, left_cols].bitcast(FP8X4),
                lhsT_scale=left[1][:, left_cols],
                rhs=codes.bitcast(FP8X4),
                rhs_scale=scales,
                start=start,
                stop=stop,
            )

        x_sc = tile("x_sc", [P, T], U8)
        xs = tile("xs", [P, PASSES * S], U8)
        w2_sc = tile("w2_sc", [P, N], U8)
        for cleared in (x_sc[32:64, :], x_sc[64:P, :], xs[:], w2_sc[:]):
            nc.gpsimd.memset(cleared.bitcast(I32), 0)

        offs_sb = sb.tile([P, S // PER_COLUMN], U16, name="offs_sb")
        pos_sb = [sb.tile([P, V // PER_COLUMN], U16, name=f"pos_sb{d}") for d in range(D)]
        w3_raw = [tile(f"w3_raw{e}", [P, PACK // 2, H], F32) for e in range(2)]
        a_raw = [tile(f"a_raw{d}", [P, PACK, V], F32) for d in range(D)]
        w1_raw = [tile(f"w1_raw{z}", [P, PACK, H], F32) for z in range(PASSES)]
        x_wd = [tile(f"x_wd{z}", [P, T], I32) for z in range(PASSES)]
        xs_rows = tile("xs_rows", [P, S], U8)
        w2_wd = tile("w2_wd", [P, N], I32)

        def load_rows(dst, src):
            nc.sync.dma_start(out=dst[:], in_=src.rearrange("(p j) c -> p j c", j=PACK))

        def load_words(z):
            nc.sync.dma_start(out=x_wd[z][:], in_=x_words[z].rearrange("p n t -> p (n t)").bitcast(I32))

        nc.sync.dma_start(out=x_sc[0:32, :].bitcast(I32), in_=x_scales.bitcast(I32).rearrange("z r n -> r z n"))
        nc.sync.dma_start(offs_sb[:], offs)
        nc.vector.tensor_copy(xs_rows[:], x_sc[:].indirect(offs_sb[:]))
        load_rows(w1_raw[0], w1[0:K_PASS, :])
        load_words(0)
        for q in range(QUADRANTS):
            nc.sync.dma_start(
                out=xs[32 * q : 32 * q + 4, :].bitcast(I32).rearrange("r (z n) -> r z n", z=PASSES),
                in_=xs_rows[8 * q : 8 * (q + 1), :].bitcast(I32),
            )
        load_rows(w1_raw[1], w1[K_PASS : 2 * K_PASS, :])
        load_words(1)
        for e in range(2):
            nc.sync.dma_start(out=w3_raw[e][:], in_=w3.rearrange("(p j) c -> p j c", j=PACK)[:, 2 * e : 2 * e + 2, :])
        nc.sync.dma_start(pos_sb[0][:], pos1)
        nc.sync.dma_start(pos_sb[1][:], pos2)
        for d in range(D):
            load_rows(a_raw[d], aT[:, V * d : V * (d + 1)])
        nc.sync.dma_start(out=w2_wd[:], in_=w2_words[0].rearrange("p n t -> p (n t)").bitcast(I32))
        for q in range(QUADRANTS):
            nc.sync.dma_start(
                out=w2_sc[32 * q : 32 * q + 4, :].bitcast(I32), in_=w2_scales[0, 4 * q : 4 * q + 4, :].bitcast(I32)
            )

        def weights(name, raw):
            src = raw[:].rearrange("p j (m t) -> p m j t", t=PACK)
            grouped = [tile(f"{name}_g{u}", [P, 2, P, PACK], BF16) for u in range(2)]
            dst = [g[:].rearrange("p t m j -> p m j t") for g in grouped]
            nc.vector.tensor_copy(dst[0], src[:, :, :, 0:2])
            nc.scalar.copy(dst[1], src[:, :, :, 2:4])
            return [quantise(f"{name}_q{u}", grouped[u][:].rearrange("p t m j -> p (t m j)")) for u in range(2)]

        xw = [tile(f"xw{z}", [P, S], U32) for z in range(PASSES)]
        h = tile("h", [P, PACK, S], F32)
        groups = [(0, range(0, 2)), (0, range(2, PACK))] + [(e, range(PACK)) for e in range(1, QUARTERS)]
        h_ps = [psum.tile([P, len(rows), P], F32, name=f"h_ps{n}", tag=f"bank{n}") for n, (e, rows) in enumerate(groups)]
        for z in range(PASSES):
            last = z == PASSES - 1
            w1_q = weights(f"w1{z}", w1_raw[z])
            window = x_wd[z][:].bitcast(U32)
            if not last:
                nc.vector.tensor_copy(xw[z][:], window.indirect(offs_sb[:]))
            for bank, (e, rows) in zip(h_ps, groups):
                cols = piece(e)
                if last and rows.start == 0:
                    nc.vector.tensor_copy(xw[z][:, cols], window.indirect(entries(offs_sb, cols)))
                for t in rows:
                    product(
                        bank[:, t - rows.start, :],
                        w1_q[t // 2],
                        piece(t % 2),
                        xw[z][:, cols],
                        xs[:, S * z + cols.start : S * z + cols.stop],
                        z == 0 and t == rows.start,
                        last and t == rows.stop - 1,
                    )
                if last:
                    nc.scalar.activation(h[:, rows.start : rows.stop, cols], bank[:], SILU)

        w3_g = tile("w3_g", [P, PACK, P, PACK], BF16)
        w3_dst = w3_g[:].rearrange("p t m j -> p m t j")
        w3_src = [raw[:].rearrange("p j (m t) -> p m t j", t=PACK) for raw in w3_raw]
        nc.vector.tensor_copy(w3_dst[:, :, :, 0:2], w3_src[0])
        for u in range(2):
            nc.vector.tensor_copy(w3_dst[:, :, 2 * u : 2 * u + 2, 2:4], w3_src[1][:, :, 2 * u : 2 * u + 2, :])
        w3_q = [
            quantise(f"w3_q{u}", w3_g[:, 2 * u : 2 * u + 2].rearrange("p t m j -> p (t m j)")) for u in range(2)
        ]

        whole = slice(0, V)
        every = slice(0, PACK)
        a_g = [[tile(f"a_g{d}{s}", [P, P, PACK], BF16) for s in range(HALVES)] for d in range(D)]
        z_g = [tile(f"z_g{s}", [P, P, PACK], BF16) for s in range(HALVES)]
        f_ps = {}

        def window(d, t, cols):
            return h[:, t, :].indirect(entries(pos_sb[d], cols))

        def round_angles(d, s):
            nc.vector.tensor_copy(
                a_g[d][s][:].rearrange("p (c i) j -> p c j i", i=RUN),
                a_raw[d][:, :, piece(s)].rearrange("p j (c i) -> p c j i", i=RUN),
            )

        def filters(d, s):
            codes, scales = quantise(f"a_q{d}{s}", a_g[d][s][:].rearrange("p c j -> p (c j)"))
            f_ps[d, s] = psum.tile([P, PACK, P], F32, name=f"f_ps{d}{s}", tag=f"bank{QUARTERS + 2 * d + s}")
            for t in range(PACK):
                product(f_ps[d, s][:, t, :], w3_q[t // 2], piece(t % 2), codes[:], scales[:], True, True)

        def multiply(d, s, picked, rows):
            nc.vector.tensor_tensor(prod[d][s][:, rows, :], picked[:, rows, :], f_ps[d, s][:, rows, :], MULT)

        def add(s, cols):
            nc.vector.tensor_tensor(
                z_g[s][:, cols, :].rearrange("p (c i) t -> p c t i", i=RUN),
                prod[0][s][:, :, cols].rearrange("p t (c i) -> p c t i", i=RUN),
                prod[1][s][:, :, cols].rearrange("p t (c i) -> p c t i", i=RUN),
                ADD,
            )

        def project(s, parts):
            codes = tile(f"z_codes{s}", [P, P], U32)
            scales = tile(f"z_scales{s}", [P, P], U8)
            for cols in parts:
                nc.vector.quantize_mx(
                    out=codes[:, cols].bitcast(FP8X4),
                    scales=scales[:, cols],
                    in_=z_g[s][:, cols, :].rearrange("p v t -> p (v t)"),
                )
            o_sb = tile(f"o_sb{s}", [P, P], F32)
            for n, cols in enumerate(parts):
                o_ps = psum.tile([P, cols.stop - cols.start], F32, name=f"o_ps{s}{n}", tag=f"bank{s + n}")
                product(o_ps[:], (w2_wd, w2_sc), piece(0), codes[:, cols], scales[:, cols], True, True)
                nc.scalar.activation(o_sb[:, cols], o_ps[:], SILU)
            nc.sync.dma_start(out=out[:, piece(s)], in_=o_sb[:])

        first = tile("first", [P, PACK, V], F32, tag="w3_raw1")
        second = tile("second", [P, PACK, V], F32)
        nc.vector.tensor_copy(first[:, 0, :], window(0, 0, whole))
        for t in range(1, PACK):
            nc.scalar.activation(first[:, t, :], window(0, t, whole), COPY)
        ends = [slice(P, P + P // 2), slice(P + P // 2, V)]
        order = [(t, piece(s)) for s in range(HALVES) for t in range(PACK)][:-1]
        for t, cols in order + [(PACK - 1, cols) for cols in ends]:
            nc.scalar.activation(second[:, t, cols], window(1, t, cols), COPY)
        for d in range(D):
            for s in range(HALVES):
                round_angles(d, s)
            for s in range(HALVES):
                filters(d, s)
        first_prod = tile("first_prod", [P, HALVES, PACK, P], F32, tag="a_raw1")
        prod = [[first_prod[:, s] for s in range(HALVES)], [tile(f"prod{s}", [P, PACK, P], F32)[:] for s in range(HALVES)]]
        multiply(0, 0, first[:, :, piece(0)], every)
        multiply(0, 1, first[:, :, piece(1)], every)
        multiply(1, 0, second[:, :, piece(0)], slice(0, PACK - 1))
        multiply(1, 0, second[:, :, piece(0)], slice(PACK - 1, PACK))
        add(0, piece(0))
        multiply(1, 1, second[:, :, piece(1)], slice(0, PACK // 2))
        project(0, [piece(0)])
        multiply(1, 1, second[:, :, piece(1)], slice(PACK // 2, PACK - 1))
        inner = [slice(0, P // 2), slice(P // 2, P)]
        for cols, here in zip(ends, inner):
            nc.vector.tensor_tensor(
                prod[1][1][:, PACK - 1, here], second[:, PACK - 1, cols], f_ps[1, 1][:, PACK - 1, here], MULT
            )
        for here in inner:
            add(1, here)
        project(1, inner)
